import numpy as np, ml_dtypes
CORES = [35,38,43,46]
N = 4
BF = ml_dtypes.bfloat16
W, L, M, P, Q, F, RO = 4096, 32, 4, 16, 32, 4, 2
CAP = (N - 1) * Q
def look(u, m):
    return (u * (u >> 5) + (2 * m + 1) * u) & (W - 1)
def pick(x, ix):
    return np.take_along_axis(x, ix[..., None, :], -1)
def pack(x, w, th):
    return {"x0": np.ascontiguousarray(x.reshape(N, 128, W)).astype(np.float32).astype(BF), "wt": np.ascontiguousarray(w).reshape(N, 128, 1).astype(np.float32).astype(BF),
            "th": np.repeat(th, 16, axis=1).astype(np.int32)}
def texture(rng):
    x = np.empty((N, 8, 16, W), np.int64); stock = rng.permutation(np.array([8, 24, 60, 120, 200, 300, 400, 600]))
    for g in range(8):
        n = int(stock[g]); base = rng.integers(0, 256, (n, 16))
        for q in range(N):
            e = 1.5 + rng.random()
            x[q, g] = (base[np.minimum((n * rng.random(W) ** e).astype(np.int64), n - 1)] + rng.integers(-2, 3, (W, 16))).T
    return np.clip(x, 0, 255)
def far(rng):
    return rng.integers(0, 256, (N, 8, 16, W))
def weights(rng):
    w = rng.integers(0, 256, (8, 16)); w[:, 0] = 1; w[:, 1] = 16; w[:, 13:] = 0
    return w
def with_hash(rng, w, u):
    k = rng.integers(0, 256, (len(u), 16)); v = (u - k[:, 2:] @ w[2:]) & (W - 1)
    k[:, 0] = v & 15; k[:, 1] = v >> 4
    return k
def odd(rng, m, n):
    u = np.arange(1, W, 2); u = rng.permutation(u[((u >> 5) & 1) == 0])
    i = np.unique(look(u, m), return_index=True)[1]
    assert len(i) >= n
    return rng.permutation(u[i])[:n]
def runs(rng):
    r = W // (L + F); n = min(r, CAP + 12)
    return L * np.sort(rng.permutation(r)[:n]) + L - 2
def setup_inputs(rng):
    return pack(texture(rng), rng.integers(0, 256, (N, 8, 16)), rng.integers(20, 41, (N, 8, 2)))
def setup_inputs_room(rng):
    x = far(rng); w = weights(rng); th = np.stack([rng.integers(1, 60, (N, 8)), rng.choice(np.array([1, 2, 40]), (N, 8))], axis=-1)
    th[rng.integers(0, N), rng.integers(4, 6), 1] = 0
    for g in range(8):
        m = g % M; p = runs(rng); n = len(p); u = odd(rng, m, n); c = look(u, m); k = with_hash(rng, w[g], u)
        for q in range(N):
            a = int(rng.choice(np.array([0, 1, CAP - 1, CAP, CAP + 1, n])))
            if q == 0: a = (CAP, CAP + 1, n, CAP - 1, 1, 0, CAP, CAP + 1)[g]
            i = rng.permutation(n)[:a]
            x[q, g][:, c] = k.T; x[q, g][:, p[i]] = k[i].T
    return pack(x, np.broadcast_to(w, (N, 8, 16)), th)
def setup_inputs_ties(rng):
    x = far(rng); w = weights(rng); t = rng.integers(2, 250, 8); t2 = t + rng.integers(-1, 2, (N, 8))
    for g in range(1, 8, 2):
        a = 4 * int(rng.integers(65, 124)) + g % 4; t2[:, g] = a; t[g] = a + int(rng.integers(0, 2))
    th = np.stack([np.broadcast_to(t, (N, 8)), t2], axis=-1)
    for g in range(8):
        m = g % M; p = runs(rng); n = len(p); u = odd(rng, m, n); k = with_hash(rng, w[g], u); k[:, 13:] = 0; more = 255 * (g % 2)
        for q in range(N):
            for c in (look(u, m + 1), look(u, m)):
                z = k + 0; z[:, 14] = rng.integers(0, 3, n); x[q, g][:, c] = z.T
            z = k + 0; z[:, 13] = more; z[:, 15] = t[g] - more + rng.integers(-2, 1, n); x[q, g][:, p] = z.T
    return pack(x, np.broadcast_to(w, (N, 8, 16)), th)
def over_the_end(rng, x, w, g):
    p = W - L - 2; every = np.arange(W); first = look(every, 0); later = look(every, np.arange(1, P)[:, None])
    good = (first >= L) & (first < p - L)
    j, uk = np.nonzero((later > W - F) & good & ~np.any(later == p, axis=0))
    i = int(rng.integers(0, len(uk))); u = int(uk[i]); c1 = int(first[u]); c2 = int(later[j[i], u])
    a = int(rng.choice(every[good & (first != c1)])); ca = int(first[a])
    k = with_hash(rng, w[g], np.array([u]))[0]; k[15] = 0; near = k + 0; near[15] = 3
    ka = with_hash(rng, w[g], np.full(N, a))
    for q in range(N):
        x[q, g][:, [0, ca]] = ka[q][:, None]; x[q, g][:, c1] = near; x[q, g][:, [p, c2 - F]] = k[:, None]
def setup_inputs_ends(rng):
    x = far(rng); w = weights(rng); th = rng.integers(1, 60, (N, 8, 2))
    mm, uu = np.nonzero(look(np.arange(W), np.arange(M)[:, None]) >= W - L // 2)
    for g in range(8):
        if g % 4 == 3:
            over_the_end(rng, x, w, g); th[:, g] = rng.integers(4, 60, (N, 2))
            continue
        if g % 2 == 0:
            o = rng.permutation(len(uu)); c, i = np.unique(look(uu[o], mm[o]), return_index=True); u = uu[o][i]; p = L * rng.permutation(len(u))
        else:
            u = odd(rng, g % M, 1); c = look(u, g % M); p = np.array([W - 2])
        k = with_hash(rng, w[g], u)
        for q in range(N):
            x[q, g][:, c] = k.T; x[q, g][:, p] = k.T
    return pack(x, np.broadcast_to(w, (N, 8, 16)), th)
def setup_inputs_alike(rng):
    x = texture(rng); w = rng.integers(0, 256, (N, 8, 16)); th = rng.integers(20, 41, (N, 8, 2))
    for g in range(0, 8, 2):
        base = rng.integers(0, 256, (4, 16)); x[:, g] = base[rng.integers(0, 4, (N, W))].transpose(0, 2, 1)
    th[:, 0] = 1; th[:, 2] = 4096; th[:, 4, 0] = 0; th[:, 1, 0] = 4096; th[:, 1, 1] = 0; th[:, 3, 1] = 4096
    w[:, 6] = 0; w[:, 5] = 255
    x[:, 1, :, 0] = 255
    w[:, 7] = rng.integers(230, 256, (N, 16))
    up = rng.random((N, 1, W)) < 0.5; up[::2] = False
    x[:, 7] = np.where(up, 255 - rng.integers(0, 40, (N, 16, W)), rng.integers(0, 40, (N, 16, W)))
    for q in range(N):
        x[q, 1][:, L * (1 + rng.permutation(W // L - 1)[:W // L // 2])] = 0
        if q % 2 == 0:
            th[q, 7, 0] = rng.integers(150, 260); th[q, 7, 1] = rng.integers(3100, 3600)
        else:
            th[q, 7, 0] = rng.integers(2048, 3000); th[q, 7, 1] = rng.integers(100, 4097)
            c = look((255 * int(np.sum(w[q, 7]))) & (W - 1), 0); x[q, 7][:, [0, L, c]] = 255
    th[0, 7, 1] = 4096
    return pack(x, w, th)
def setup_inputs_spread(rng):
    x = np.minimum((np.exp2(8 * rng.random((N, 8, 1, W))) * rng.random((N, 8, 16, W))).astype(np.int64), 255)
    w = np.minimum(np.exp2(8 * rng.random((N, 8, 16))).astype(np.int64), 255) * (rng.random((N, 8, 16)) > 0.0625)
    return pack(x, w, np.minimum(np.exp2(12 * rng.random((N, 8, 2))).astype(np.int64), 4096))
def check_inputs(d):
    bad = []
    for k in ("x0", "wt"):
        v = np.asarray(d[k]).astype(np.float32)
        if not np.all((v >= 0) & (v <= 255) & (v == np.floor(v))): bad.append("whole numbers of " + k)
    v = np.asarray(d["th"])
    if np.min(v) < 0 or np.max(v) > 4096: bad.append("range of th")
    v = v.reshape(N, 8, 16, 2)
    if np.any(v != v[:, :, :1]): bad.append("rows of th alike in a group")
    return bad
def reference(x0, wt, th):
    x = x0.astype(np.float32).astype(np.int64).reshape(N, 8, 16, W); w = wt.astype(np.float32).astype(np.int64).reshape(N, 8, 16, 1)
    t = th.astype(np.int64).reshape(N, 8, 16, 2)[:, :, 0]; here = np.arange(W)
    for rnd in range(RO):
        u = np.add.reduce(w * x, axis=2) & (W - 1)
        nx = np.zeros_like(u) + ((here + 1) & (W - 1))
        for m in range(M - 1, -1, -1):
            c = look(u, m); near = np.add.reduce(np.abs(pick(x, c) - x), axis=2) < t[..., :1]
            nx = np.where(near, (c + 1) & (W - 1), nx)
        s = np.zeros((N, 8, W // L, L), np.int64); s[..., 0] = L * np.arange(W // L)
        for k in range(1, L): s[..., k] = np.take_along_axis(nx, s[..., k - 1], -1)
        jump = np.zeros(s.shape, bool); jump[..., :-1] = s[..., 1:] != ((s[..., :-1] + 1) & (W - 1))
        s = s.reshape(N, 8, W); jump = jump.reshape(N, 8, W)
        site = np.argsort(~jump, axis=-1, kind="stable")[..., :CAP]
        live = np.take_along_axis(jump, site, -1); ask = pick(x, np.take_along_axis(s, site, -1))
        found = np.zeros((N, 8, CAP), bool); fill = np.zeros((N, 8, 16, CAP, F), np.int64)
        for q in range(N):
            for d in range(1, N):
                b = (q + d) % N; cut = slice((d - 1) * Q, d * Q); a = ask[q][:, :, cut]
                v = np.add.reduce(w[b] * a, axis=1) & (W - 1); c = look(v[..., None], np.arange(P))
                off = np.add.reduce(np.abs(pick(x[b], c.reshape(8, -1)).reshape(8, 16, Q, P) - a[..., None]), axis=1)
                best = np.take_along_axis(c, np.argmin(off, axis=-1)[..., None], -1)
                found[q][:, cut] = np.min(off, axis=-1) < t[b][:, 1:]
                fill[q][:, :, cut] = pick(x[b], ((best + 1 + np.arange(F)) & (W - 1)).reshape(8, -1)).reshape(8, 16, Q, F)
        found = found & live
        more = np.zeros((N, 8, W), np.int64); np.put_along_axis(more, site, found.astype(np.int64) * F, -1)
        place = here + np.add.accumulate(more, axis=-1) - more
        z = np.zeros((N, 8, 16, W + F * CAP + 1), np.int64)
        np.put_along_axis(z, place[:, :, None], pick(x, s), -1)
        at = np.take_along_axis(place, site, -1)[..., None] + 1 + np.arange(F)
        at = np.where(found[..., None], at, W + F * CAP).reshape(N, 8, 1, CAP * F)
        np.put_along_axis(z, at, fill.reshape(N, 8, 16, CAP * F), -1)
        x = np.ascontiguousarray(z[..., :W])
    return {"y": x.reshape(N, 128, W).astype(np.float32).astype(BF)}

@@ -1,0 +1,690 @@
+import numpy as np
+from concourse.bass import DstId, RemoteDMATransfer
+from concourse.mybir import dt, AluOpType as OP, AxisListType, ActivationFunctionType as AF
+
+W = 4096
+RO = 2
+XW = 5184
+F32, BF, I32, U16, F16 = "float32", "bfloat16", "int32", "uint16", "float16"
+SEGS = [(0, 192), (192, 256)]
+
+SCRATCH = {}
+PLACE = {}
+
+
+def _buf(where, cols, dtype, *names):
+    for n in names:
+        SCRATCH[n] = (where, [128, cols], dtype)
+        PLACE[n] = (n, 0, cols)
+
+
+def _pack(cols, dtype, host, *names):
+    SCRATCH[host] = ("sbuf", [128, cols * len(names)], dtype)
+    for i, n in enumerate(names):
+        PLACE[n] = (host, cols * i, cols)
+
+
+_buf("sbuf", XW, BF, "XA", "XB")
+_buf("sbuf", W, BF, "Y0", "XR00", "XR01", "XR02", "XR10", "XR11", "XR12")
+_buf("sbuf", W, F32, "NX1", "NX2")
+_buf("sbuf", 1024, BF, "DD0", "DD1", "DD2", "DD3", "GA0", "GA1", "AB0", "AB1")
+_pack(256, I32, "hI", "CC3", "QI", "DI", "KI", "NXI", "UI", "HI")
+_pack(256, U16, "hU", "CL3", "NXL", "SRL")
+_pack(256, F32, "hF", "CN0", "CN1", "CN2", "CN3", "QF", "DEF", "K2", "SB", "FF", "CU", "WD", "SR", "KEY0", "KEY1")
+_pack(768, I32, "kI", "CCX", "TM")
+_buf("sbuf", 768, U16, "CLX")
+_buf("sbuf", 256, F16, "NXH")
+_pack(128, I32, "gI", "J15", "JG", "J7")
+_pack(128, F32, "gF", "MASK", "KEEP", "KP8", "R0", "R1", "Z0", "Z1", "TT0", "TT1")
+_pack(128, U16, "gU", "LE", "LO")
+_buf("sbuf", 640, F32, "RO0", "RO1")
+_buf("sbuf", 384, F32, "RO2", "ZOD", "MASK3", "KEEP3")
+_buf("sbuf", 512, F32, "IDV", "WTS")
+_buf("sbuf", 512, I32, "JI", "PB8")
+_buf("sbuf", 4608, F32, "SW")
+_buf("sbuf", 1312, F32, "WA", "WB")
+_buf("sbuf", 144, BF, "EZ", "EW", "EX")
+_buf("sbuf", 144, F32, "EZF")
+_buf("sbuf", 128, BF, "BB", "IDN", "NID", "LT", "UT", "LT4", "BB4", "WB0", "WB1", "WB2")
+_buf("sbuf", 2048, F16, "SEL")
+_buf("sbuf", 16, I32, "TH", "IC")
+_buf("sbuf", 16, F32, "FC")
+_buf("sbuf", 16, BF, "WT")
+_buf("sbuf", 4, F32, "PAR", "PR0", "PR1", "PR2")
+_pack(40, BF, "sB", "EB", "CX", "CS", "FB6")
+_buf("sbuf", 32, F16, "W16")
+_pack(32, F32, "sF", "TRJ", "ZE", "OF", "TR6", "M2", "F4", "F41", "T0F", "UF", "UF2", "I6", "IT6", "LV", "KM", "FD", "FS",
+      "CBF", "P1", "XF", "Q6", "FIF", "FPF")
+_pack(32, U16, "sU", "OL", "JL", "PL", "FL", "FP", "SL")
+_pack(48, I32, "sI", "BI", "VI", "JX", "RX", "PX", "WI", "U6", "H6", "M6", "CB", "FI", "PI6", "SI6", "X6")
+_pack(48, F32, "tF", "BF8", "CM8", "IN8")
+_pack(96, F32, "uF", "KN", "CD", "RR", "VM", "ZV")
+_pack(96, I32, "uI", "TI")
+_pack(96, U16, "uU", "TL")
+_pack(96, BF, "uB", "AQ", "MK", "EXB")
+_buf("sbuf", 1536, BF, "AR", "AD")
+_buf("sbuf", 384, BF, "FB")
+_buf("psum", 512, F32, "P0", "P7")
+_buf("psum", 1024, F32, "P12", "P34", "P56")
+
+NDMA = 20
+SEMAPHORES = ["sV", "sA", "sT", "sG", "par", "lpar"] + ["d%d" % i for i in range(NDMA)]
+SEMAPHORES += ["%s%d%d" % (k, r, h) for k in ("am", "ap", "aq", "lx", "lf") for r in range(RO) for h in range(2)]
+
+
+def rank_program(g, core, T, topo):
+    rank = T.rank_of(core)
+    if rank is None:
+        return
+    cores = list(T.cores)
+    N = len(cores)
+    queue = {"V": g.vector, "A": g.scalar, "P": g.tensor, "G": g, "S": g.sync}
+    qsem = {"V": "sV", "A": "sA", "P": "sT", "G": "sG"}
+    count = {}
+    known = {q: {} for q in queue}
+    snap = {}
+    log = {}
+    ndma = [0]
+
+    def v(name, lo=0, hi=None, st=1):
+        host, base, cols = PLACE[name]
+        return (host, base + lo, base + (cols if hi is None else hi), st)
+
+    def ap(x):
+        n, lo, hi, st = x
+        return T[n][:, lo:hi] if st == 1 else T[n][:, lo:hi:st]
+
+    def arg(x):
+        return ap(x) if isinstance(x, tuple) else x
+
+    def ind(win, off):
+        return ("ind", win, off)
+
+    def opnd(x):
+        if x[0] == "ind":
+            return ap(x[1]).indirect(ap(x[2]))
+        return ap(x)
+
+    def hits(a, b):
+        if a[1] <= b[0] or b[1] <= a[0]:
+            return False
+        if a[2] == b[2] and a[2] > 1 and (a[0] - b[0]) % a[2]:
+            return False
+        return True
+
+    def bank(x):
+        n, lo, hi, st = x
+        if SCRATCH[n][0] == "psum":
+            return n, lo // 512 * 512, (hi + 511) // 512 * 512, 1
+        return x
+
+    def wait(q, sem, n):
+        if known[q].get(sem, 0) >= n:
+            return
+        queue[q].wait_ge(T.sem[sem], n)
+        known[q][sem] = n
+        for k, c in snap.get((sem, n), {}).items():
+            if known[q].get(k, 0) < c:
+                known[q][k] = c
+
+    def order(q, reads, writes):
+        need = {}
+        for lst, wr in ((reads, False), (writes, True)):
+            for x in lst:
+                n, lo, hi, st = bank(x)
+                ps = SCRATCH[n][0] == "psum"
+                for a in log.get(n, ()):
+                    aq, aw = a[3], a[4]
+                    if not hits((lo, hi, st), a):
+                        continue
+                    if aq == q and q in qsem:
+                        if not (aw or wr) or (ps and q == "P"):
+                            continue
+                    elif not (aw or wr or ps):
+                        continue
+                    if need.get(a[5], 0) < a[6]:
+                        need[a[5]] = a[6]
+        for sem in sorted(need, key=lambda s: -need[s]):
+            wait(q, sem, need[sem])
+
+    def note(q, reads, writes, sem, n):
+        for lst, wr in ((reads, False), (writes, True)):
+            for x in lst:
+                nm, lo, hi, st = bank(x)
+                l = log.setdefault(nm, [])
+                if wr:
+                    l[:] = [a for a in l if not (a[0] >= lo and a[1] <= hi and (st == 1 or (a[2] == st and (a[0] - lo) % st == 0)))]
+                else:
+                    l[:] = [a for a in l if not (a[3] == q and not a[4] and a[0] >= lo and a[1] <= hi and a[2] == st and st == 1)]
+                l.append((lo, hi, st, q, wr, sem, n))
+
+    def emit(q, reads, writes, fn):
+        rd, wr = [], []
+        for x in reads:
+            if isinstance(x, tuple):
+                rd += [x[1], x[2]] if x[0] == "ind" else [x]
+        for x in writes:
+            if x[0] == "ind":
+                wr.append(x[1])
+                rd.append(x[2])
+            else:
+                wr.append(x)
+        order(q, rd, wr)
+        s = qsem[q]
+        count[s] = count.get(s, 0) + 1
+        fn(queue[q]).then_inc(T.sem[s], 1)
+        snap[(s, count[s])] = dict(known[q])
+        note(q, rd, wr, s, count[s])
+
+    def dma(q, out, in_, reads, writes):
+        order(q, reads, writes)
+        s = "d%d" % ndma[0]
+        ndma[0] += 1
+        count[s] = 16
+        queue[q].dma_start(out, in_).then_inc(T.sem[s], 16)
+        snap[(s, 16)] = dict(known[q])
+        note(q + "dma", reads, writes, s, 16)
+
+    def tt(out, a, b, op):
+        emit("V", [a, b], [out], lambda e: e.tensor_tensor(opnd(out), opnd(a), opnd(b), op))
+
+    def ts(out, a, s1, op0, s2=None, op1=None):
+        def f(e):
+            if op1 is None:
+                return e.tensor_scalar(ap(out), opnd(a), arg(s1), None, op0)
+            return e.tensor_scalar(ap(out), opnd(a), arg(s1), arg(s2), op0, op1)
+        emit("V", [a, s1, s2], [out], f)
+
+    def cp(q, out, a):
+        if q == "V":
+            emit("V", [a], [out], lambda e: e.tensor_copy(opnd(out), opnd(a)))
+        else:
+            emit("A", [a], [out], lambda e: e.activation(ap(out), opnd(a), AF.Copy))
+
+    def act(out, a, func, bias=0.0, scale=1.0):
+        emit("A", [a, bias, scale], [out], lambda e: e.activation(ap(out), opnd(a), func, bias=arg(bias), scale=arg(scale)))
+
+    def fill(out, c):
+        emit("V", [], [out], lambda e: e.memset(ap(out), c))
+
+    def scan(out, a, b, op0, op1, init=0.0):
+        emit("V", [a, b, init], [out], lambda e: e.tensor_tensor_scan(ap(out), ap(a), ap(b), arg(init), op0, op1))
+
+    def mm(out, l, r, start=True, stop=True):
+        emit("P", [l, r], [out], lambda e: e.matmul(ap(out), ap(l), ap(r), start, stop))
+
+    def iota(out, pattern, base, cm):
+        if SCRATCH[out[0]][2] == I32:
+            emit("G", [], [out], lambda e: e.iota(ap(out), pattern, base, cm))
+        else:
+            emit("G", [], [out], lambda e: e.iota(ap(out), pattern, base, cm, allow_small_or_imprecise_dtypes=True))
+
+    def ez(n, a):
+        return v(n, 15 - a, 143 - a)
+
+    def sel(a):
+        return v("SEL", 128 * a, 128 * a + 128)
+
+    AND, SHR = OP.bitwise_and, OP.logical_shift_right
+    wtq = v("WT", 0, 1)
+    dma("S", ap(wtq), T.wt[:], [], [wtq])
+    dma("A", ap(v("TH", 0, 2)), T.th[:], [], [v("TH", 0, 2)])
+    for n in ("XA", "Y0"):
+        for c in range(4):
+            x = v(n, 1024 * c, 1024 * c + 1024)
+            dma("SA"[c % 2], ap(x), T.x0[:, 1024 * c:1024 * c + 1024], [], [x])
+    iota(v("IC", 0, 1), [[1, 1]], 0, 1)
+    iota(v("JI"), [[1, 512]], 0, 0)
+    iota(v("QI"), [[16, 256]], 0, 1)
+    iota(v("PB8"), [[64, 8], [1, 4], [4, 16]], 0, 0)
+    ts(v("IC", 1, 2), v("IC", 0, 1), 15, AND)
+    ts(v("IC", 2, 3), v("IC", 0, 1), 112, AND)
+    fill(v("EZ"), 0.0)
+    fill(v("PAR", 2, 4), 0.0)
+    cp("V", v("FC", 0, 3), v("IC", 0, 3))
+    pf, p15, pg, t1 = v("FC", 0, 1), v("FC", 1, 2), v("FC", 2, 3), v("FC", 3, 4)
+    J = v("JI", 0, 128)
+    cp("V", v("PAR", 0, 1), wtq)
+    ts(v("PAR", 1, 2), v("TH", 1, 2), 16.0, OP.mult)
+    cp("V", t1, v("TH", 0, 1))
+    ts(v("EZ", 15, 143), J, pg, OP.is_equal)
+    ts(v("IDN"), J, pf, OP.is_equal)
+    ts(v("EW"), v("EZ"), wtq, OP.mult)
+    ts(v("NID"), J, pf, OP.is_equal, -1.0, OP.mult)
+    ts(v("QF"), v("QI"), pg, OP.subtract)
+    ts(v("J15"), J, 15, AND)
+    ts(v("JG"), J, 112, AND)
+    ts(v("J7"), J, 7, AND)
+    ts(v("MASK"), v("J15"), p15, OP.is_equal)
+    ts(v("BB"), v("JG"), pg, OP.is_equal)
+    ts(v("KEEP"), v("J15"), 0.0, OP.not_equal)
+    ts(v("KP8"), v("J7"), 0.0, OP.not_equal)
+    for a in range(16):
+        ts(sel(a), v("BB"), v("MASK", a, a + 1), OP.mult)
+    ts(v("DEF"), v("QF"), 32769.0, OP.add)
+    for k in range(3):
+        cp("A", v("MASK3", 128 * k, 128 * k + 128), v("MASK"))
+        cp("A", v("KEEP3", 128 * k, 128 * k + 128), v("KEEP"))
+
+    def late_constants():
+        ts(v("K2", 0, 128), v("J7"), 0.0, OP.is_gt, 2.0, OP.mult)
+        ts(v("K2", 128, 256), v("J7"), 0.0, OP.is_gt, 2.0, OP.mult)
+        ts(v("BB4"), v("JG"), pg, OP.is_equal, 4.0, OP.mult)
+        ts(v("TT0"), J, pf, OP.is_gt)
+        ts(v("TT1"), J, pf, OP.is_lt)
+        tt(v("LT"), v("TT0"), v("BB"), OP.mult)
+        tt(v("UT"), v("TT1"), v("BB"), OP.mult)
+        ts(v("LT4"), v("LT"), 4.0, OP.mult)
+        ts(v("EX"), v("EZ"), 16.0, OP.mult)
+        ts(v("EZF"), v("EZ"), 0.0625, OP.mult)
+        ts(v("LE", 0, 8), v("QF", 0, 8), 32.0, OP.mult)
+        ts(v("WTS"), v("PB8"), 4096.0, OP.mult, float(1 << 21), OP.add)
+        ts(v("IDV"), v("JI"), 8.0, OP.mult)
+        tt(v("IDV"), v("IDV"), v("WTS"), OP.add)
+        ts(v("TRJ"), v("QF", 0, 32), 4096.0, OP.add)
+        ts(v("TR6", 0, 6), v("QF", 0, 6), 4.0, OP.mult, 4800.0, OP.add)
+        ts(v("M2", 0, 16), v("JI", 0, 16), 2.0, OP.mult)
+        cp("V", v("F4", 0, 4), v("JI", 0, 4))
+        ts(v("F41", 0, 4), v("JI", 0, 4), 1.0, OP.add)
+        ts(v("TI"), v("JI", 0, 96), 1, SHR, 15, AND)
+        cp("V", v("MK"), v("TI"))
+        fill(v("EB", 0, 4), 0.0)
+        fill(v("CS", 0, 1), 0.0)
+
+    mine = topo.chip(core)
+    mate = [c for c in cores if topo.mates(topo.chip(c), mine) and topo.die(c) == topo.die(core)][0]
+    near = [c for c in cores if c != core and topo.chip(c) == mine][0]
+    diag = [c for c in cores if c not in (core, mate, near)][0]
+
+    def slot(receiver, owner):
+        return (T.rank_of(owner) - T.rank_of(receiver) - 1) % N
+
+    off = topo.engines(core, mate)
+    on = [e for e in topo.engines(core, near) if e not in off]
+
+    def dst(c):
+        a = topo.addr(c)
+        return DstId(rid=a[0], pnc=a[1])
+
+    def remote(transfers, local, reads):
+        order("G", reads, [])
+        n = sum(len(es) for _, _, _, es, _ in transfers)
+        count[local] = count.get(local, 0) + n
+        g.remote_dma_fused([RemoteDMATransfer(dst_ids=[dst(c)], dma_engine_mask=sum(1 << e for e in es), remote_sem=T.sem[rs], src=s, dst=d)
+                            for c, s, d, es, rs in transfers], local_sem=T.sem[local])
+        snap[(local, count[local])] = dict(known["G"])
+        note("Gremote", reads, [], local, count[local])
+
+    def arrives(name, lo, hi, sem, n):
+        count[sem] = n
+        note("remote", [], [v(name, lo, hi)], sem, n)
+
+    for d in range(3):
+        arrives("PR%d" % d, 0, 4, "par", 3)
+
+    def send_params():
+        remote([(c, ap(v("PAR")), T["PR%d" % slot(c, core)][:], [es], "par")
+                for c, es in ((near, on[0]), (mate, off[0]), (diag, off[1]))], "lpar", [v("PAR")])
+
+    def halves():
+        return [(h, 2048 * h, 2048 * h + 2048) for h in range(2)]
+
+    def broadcast(rd, x):
+        for h, lo, hi in halves():
+            src = v(x, lo, hi)
+            remote([(mate, ap(src), T["XR%d%d" % (rd, slot(mate, core))][:, lo:hi], off, "am%d%d" % (rd, h)),
+                    (near, ap(src), T["XR%d%d" % (rd, slot(near, core))][:, lo:hi], on, "ap%d%d" % (rd, h))], "lx%d%d" % (rd, h), [src])
+        for h, lo, hi in halves():
+            a, b, c = ("XR%d%d" % (rd, slot(core, o)) for o in (mate, near, diag))
+            arrives(a, lo, hi, "am%d%d" % (rd, h), len(off))
+            arrives(b, lo, hi, "ap%d%d" % (rd, h), len(on))
+            arrives(c, lo, hi, "aq%d%d" % (rd, h), len(on))
+
+    def hand_on(rd):
+        for h, lo, hi in halves():
+            src = v("XR%d%d" % (rd, slot(core, mate)), lo, hi)
+            remote([(near, ap(src), T["XR%d%d" % (rd, slot(near, mate))][:, lo:hi], on, "aq%d%d" % (rd, h))], "lf%d%d" % (rd, h), [src])
+
+    for rd in range(RO):
+        X, Xn = ("XA", "XB") if rd % 2 == 0 else ("XB", "XA")
+        if rd > 0:
+            for c in range(4):
+                x, y = v(X, 1024 * c, 1024 * c + 1024), v("Y0", 1024 * c, 1024 * c + 1024)
+                dma("S", ap(y), ap(x), [x], [y])
+        broadcast(rd, X)
+        if rd == 0:
+            send_params()
+        iota(v("SW", 0, 96), [[0, 96]], 0, 0)
+        iota(v("WA", 0, 1024), [[0, 1024]], 0, 0)
+        iota(v("WB", 4, 1032), [[0, 1028]], 0, 0)
+        hand_on(rd)
+        hb = ["P0", "P7"]
+        for s, (lo, hi) in enumerate(SEGS):
+            for a in range(16):
+                mm(v(hb[s], 0, hi - lo), ez("EW", a), v(X, 16 * lo + a, 16 * hi, 16), a == 0, a == 15)
+        if rd == 0:
+            late_constants()
+
+        def cl(m, lo, hi):
+            if m == 3:
+                return v("CL3", lo, hi)
+            s0, s1 = SEGS[0] if hi <= SEGS[0][1] else SEGS[1]
+            o = 3 * s0 + m * (s1 - s0) - s0
+            return v("CLX", o + lo, o + hi)
+
+        def looks(s):
+            lo, hi = SEGS[s]
+            w = hi - lo
+            u, hm, u2 = v("UI", 0, w), v(hb[s], w, 2 * w), v(hb[s], 0, w)
+            t = [v("TM", m * w, m * w + w) for m in range(3)]
+            cp("V", u, v(hb[s], 0, w))
+            ts(u, u, W - 1, AND)
+            ts(v("HI", 0, w), u, 5, SHR)
+            ts(hm, v("HI", 0, w), 7.0, OP.add)
+            tt(t[0], hm, u, OP.mult)
+            ts(v("CC3", lo, hi), t[0], W - 1, AND)
+            cp("V", v("CL3", lo, hi), v("CC3", lo, hi))
+            ts(hm, v("HI", 0, w), 1.0, OP.add)
+            tt(t[0], hm, u, OP.mult)
+            ts(u2, u, 2.0, OP.mult)
+            tt(t[1], u2, t[0], OP.add)
+            tt(t[2], u2, t[1], OP.add)
+            c = (3 * lo, 3 * hi)
+            ts(v("CCX", *c), v("TM", 0, 3 * w), W - 1, AND)
+            cp("V", v("CLX", *c), v("CCX", *c))
+
+        def keys(s):
+            lo, hi = SEGS[s]
+            w = hi - lo
+            for m in range(3):
+                ts(v("CN%d" % m, lo, hi), v("CCX", 3 * lo + m * w, 3 * lo + m * w + w), float(1 + 8192 * m), OP.add)
+            ts(v("CN3", lo, hi), v("CC3", lo, hi), float(1 + 8192 * 3), OP.add)
+
+        dn, an, kn = [0], [0], [0]
+
+        def dist(m, s):
+            lo, hi = SEGS[s]
+            w = hi - lo
+            if s == 0:
+                o = 512 * (m // 2) + w * (m % 2)
+                return v("P12", o, o + w)
+            return v("P34", 0, w) if m == 2 else v("P0", 64 * (m % 3) + 128 * (m // 3), 64 * (m % 3) + 128 * (m // 3) + w)
+
+        def reduce_abs(m, q, buf):
+            s = 0 if 64 * q + 64 <= SEGS[0][1] else 1
+            n, o, _, _ = dist(m, s)
+            o += 64 * q - SEGS[s][0]
+            for a in range(16):
+                mm((n, o, o + 64, 1), ez("EZ", a), v(buf, a, 1024, 16), a == 0, a == 15)
+
+        def vgather(m, q):
+            b = "DD%d" % (dn[0] % 4)
+            dn[0] += 1
+            tt(v(b), ind(v(X, 0, W), cl(m, 64 * q, 64 * q + 64)), v("Y0", 1024 * q, 1024 * q + 1024), OP.subtract)
+            return b
+
+        def aabs(m, q, b):
+            act(v(b), v(b), AF.Abs)
+            reduce_abs(m, q, b)
+
+        def agather(q):
+            b = "GA%d" % (an[0] % 2)
+            for k in range(2):
+                mm(v("P34", 512 * k, 512 * k + 512), v("NID"), v(X, 1024 * q + 512 * k, 1024 * q + 512 * k + 512), True, False)
+            cp("A", v(b), ind(v(X, 0, W), cl(3, 64 * q, 64 * q + 64)))
+            for k in range(2):
+                mm(v("P34", 512 * k, 512 * k + 512), v("IDN"), v(b, 512 * k, 512 * k + 512), False, True)
+
+        def aabs3(q):
+            b = "AB%d" % (an[0] % 2)
+            an[0] += 1
+            act(v(b), v("P34"), AF.Abs)
+            reduce_abs(3, q, b)
+
+        def nearest(s, ms, first, last):
+            lo, hi = SEGS[s]
+            w = hi - lo
+            o = (lo, hi)
+            pen, run = v("P56", 0, w), v("P56", 512, 512 + w)
+            for m in ms:
+                key = v("KEY%d" % (kn[0] % 2), 0, w)
+                kn[0] += 1
+                ts(pen, dist(m, s), t1, OP.is_ge, 65536.0, OP.mult)
+                tt(key, pen, v("CN%d" % m, *o), OP.add)
+                tt(v("KI", *o) if last and m == ms[-1] else run, v("DEF", *o) if first and m == ms[0] else run, key, OP.min)
+            if last:
+                ts(v("NXI", *o), v("KI", *o), W - 1, AND)
+                ts(v("NXH", *o), v("NXI", *o), -2048.0, OP.add)
+                cp("V", v("NXL", *o), v("NXI", *o))
+                banks = [("P56", 0), ("P56", 512), ("P7", 0)]
+                per = 512 // w
+                for i in range(0, 16, per):
+                    bn, b0 = banks[i // per % 3]
+                    for j in range(per):
+                        mm(v(bn, b0 + w * j, b0 + w * j + w), sel(i + j), v("NXH", *o))
+                    for j in range(per):
+                        cp("VA"[i // per % 2], v("NX1", 16 * lo + i + j, 16 * hi, 16), v(bn, b0 + w * j, b0 + w * j + w))
+
+        looks(0)
+        agather(0)
+        aabs(0, 0, vgather(0, 0))
+        aabs3(0)
+        agather(1)
+        keys(0)
+        aabs(0, 1, vgather(0, 1))
+        aabs3(1)
+        aabs(0, 2, vgather(0, 2))
+        looks(1)
+        keys(1)
+        agather(2)
+        aabs(1, 0, vgather(1, 0))
+        aabs3(2)
+        aabs(1, 1, vgather(1, 1))
+        aabs(1, 2, vgather(1, 2))
+        aabs(2, 0, vgather(2, 0))
+        aabs(2, 1, vgather(2, 1))
+        agather(3)
+        aabs(2, 2, vgather(2, 2))
+        aabs3(3)
+        nearest(0, (0, 1), True, False)
+        aabs(0, 3, vgather(0, 3))
+        nearest(0, (3, 2), False, True)
+        aabs(1, 3, vgather(1, 3))
+        aabs(2, 3, vgather(2, 3))
+        nearest(1, (3, 0, 1, 2), True, True)
+        cp("V", v("NX2", 0, 2048), ind(v("NX1"), v("NXL", 0, 128)))
+        cp("A", v("NX2", 2048, 4096), ind(v("NX1"), v("NXL", 128, 256)))
+
+        def y0(k):
+            l = v("LE" if k % 2 == 0 else "LO", 8 * (k // 2), 8 * (k // 2) + 8)
+            cp("A", v("Y0", k, W, 32), ind(v(X, 0, W), l))
+
+        def sb_of(k):
+            return v("SB", k, 256, 32)
+
+        def odd_by_tensor(j, pb, ro):
+            cp("A", v(ro), ind(v("NX1"), v("LE", 8 * j, 8 * j + 40)))
+            for a in range(16):
+                mm(v(pb, 0, 40), ez("EZF", a), v(ro, a, 640, 16), a == 0, a == 15)
+
+        def odd_done(j, pb):
+            ts(v("LO", 8 * j, 8 * j + 40), v(pb, 0, 40), 2048.0, OP.add)
+            for k in range(5):
+                cp("A", sb_of(2 * (j + k) + 1), v(pb, 8 * k, 8 * k + 8))
+
+        def odd_by_vector(j):
+            tt(v("RO2"), ind(v("NX1"), v("LE", 8 * j, 8 * j + 24)), v("MASK3"), OP.mult)
+            scan(v("ZOD"), v("KEEP3"), v("RO2"), OP.mult, OP.add)
+            ts(v("LO", 8 * j, 8 * j + 24), v("ZOD", 15, 384, 16), 2048.0, OP.add)
+            for k in range(3):
+                cp("V", sb_of(2 * (j + k) + 1), v("ZOD", 128 * k + 15, 128 * k + 128, 16))
+
+        for i in range(16):
+            le = v("LE", 8 * i, 8 * i + 8)
+            if i < 15:
+                r, z = v("R%d" % (i % 2)), "Z%d" % (i % 2)
+                tt(r, ind(v("NX2"), le), v("MASK"), OP.mult)
+                scan(v(z), v("KEEP"), r, OP.mult, OP.add)
+                ts(v("LE", 8 * i + 8, 8 * i + 16), v(z, 15, 128, 16), 2048.0, OP.add)
+            if i == 4:
+                odd_by_tensor(0, "P0", "RO0")
+            if i == 9:
+                odd_by_tensor(5, "P7", "RO1")
+            y0(2 * i)
+            if i == 11:
+                odd_done(0, "P0")
+                for k in range(5):
+                    y0(2 * k + 1)
+            if i == 12:
+                odd_by_vector(10)
+        odd_done(5, "P7")
+        odd_by_vector(13)
+        for b in range(8):
+            ts(v("SB", 32 * b, 32 * b + 32, 2), v("LE", b, 128, 8), -2048.0, OP.add)
+        for k in range(5, 16):
+            y0(2 * k + 1)
+        tt(v("DI", 0, 255), v("SB", 1, 256), v("SB", 0, 255), OP.subtract)
+        ts(v("DI", 0, 255), v("DI", 0, 255), W - 1, AND)
+        ts(v("FF", 0, 255), v("DI", 0, 255), 1.0, OP.not_equal)
+        fill(v("FF", 31, 256, 32), 0.0)
+        scan(v("CU"), v("FF"), v("FF"), OP.add, OP.max)
+        scan(v("WD"), v("K2"), v("FF"), OP.mult, OP.add)
+        for k in range(4):
+            cp("V", v("EB", 4 + k, 36, 4), v("CU", 31, 256, 32))
+        tt(v("CX", 0, 32), v("CU", 0, 256, 8), v("FF", 0, 256, 8), OP.subtract)
+        first = v("P12", 0, 32)
+        mm(first, v("LT"), v("EB", 4, 36), True, False)
+        mm(first, v("UT"), v("EB", 0, 32), False, False)
+        mm(first, v("IDN"), v("CX", 0, 32), False, True)
+        cp("V", v("W16"), v("WD", 7, 256, 8))
+        for a in range(16):
+            mm(v("P12", 512 + a, 1024, 16), sel(a), v("W16"))
+        cp("A", v("WTS"), v("P12", 512, 1024))
+        mm(v("P0", 0, 1), v("BB"), v("EB", 35, 36))
+        ts(v("ZE"), v("WD", 7, 256, 8), 0.0, OP.is_equal)
+        tt(v("ZE"), v("ZE"), v("TRJ"), OP.mult)
+        tt(v("OF"), first, v("ZE"), OP.max)
+        cp("V", v("OL"), v("OF"))
+        cp("V", ind(v("SW"), v("OL")), v("IDV"))
+        ts(v("KN"), v("SW", 0, 96), 0.0, OP.is_equal)
+        scan(v("CD"), v("KN"), v("SW", 0, 96), OP.mult, OP.add)
+        scan(v("RR"), v("KN"), v("KN"), OP.mult, OP.add)
+        tt(v("VM"), v("CD"), v("RR"), OP.add)
+        tt(v("VM"), v("VM"), v("MASK", 0, 96), OP.mult)
+        scan(v("ZV"), v("KEEP", 0, 96), v("VM"), OP.mult, OP.add)
+        cp("V", v("VI", 0, 6), v("ZV", 15, 96, 16))
+        ts(v("JX", 0, 6), v("VI", 0, 6), 3, SHR, 511, AND)
+        ts(v("RX", 0, 6), v("VI", 0, 6), 7, AND)
+        cp("V", v("JL", 0, 6), v("JX", 0, 6))
+        ts(v("PX", 0, 6), v("VI", 0, 6), 12, SHR, 511, AND)
+        tt(v("VM"), ind(v("WTS"), v("JL", 0, 6)), v("MASK", 0, 96), OP.mult)
+        ts(v("Q6", 0, 6), v("PX", 0, 6), 8.0, OP.mult)
+        scan(v("ZV"), v("KEEP", 0, 96), v("VM"), OP.mult, OP.add)
+        ts(v("LV", 0, 6), v("QF", 0, 6), v("P0", 0, 1), OP.is_lt)
+        cp("V", v("WI", 0, 6), v("ZV", 15, 96, 16))
+        for k in range(8):
+            ts(v("BI", k, 48, 8), v("WI", 0, 6), 7 - k, SHR, 1, AND)
+        cp("V", v("BF8"), v("BI"))
+        tt(v("BF8", 0, 48, 8), v("BI", 0, 48, 8), v("RX", 0, 6), OP.subtract)
+        scan(v("CM8"), v("KP8", 0, 48), v("BF8"), OP.mult, OP.add)
+        ts(v("IN8"), v("CM8"), 0.0, OP.is_le)
+        scan(v("CM8"), v("KP8", 0, 48), v("IN8"), OP.mult, OP.add)
+        tt(v("I6", 0, 6), v("Q6", 0, 6), v("CM8", 7, 48, 8), OP.add)
+        ts(v("PL", 0, 6), v("I6", 0, 6), 4095.0, OP.min)
+        cp("V", v("AQ"), ind(v("Y0"), v("PL", 0, 6)))
+        if rd == 0:
+            for d in range(3):
+                ts(v("WB%d" % d), v("BB"), v("PR%d" % d, 0, 1), OP.mult)
+        for d in range(3):
+            mm(v("P7", 32 * d, 32 * d + 32), v("WB%d" % d), v("AQ", 32 * d, 32 * d + 32))
+        for d in range(3):
+            o = 512 * d
+            cp("A", v("AR", o, o + 32), v("AQ", 32 * d, 32 * d + 32))
+            for w in (32, 64, 128, 256):
+                cp("A", v("AR", o + w, o + 2 * w), v("AR", o, o + w))
+        ts(v("IT6", 0, 6), v("I6", 0, 6), 1.0, OP.add)
+        tt(v("IT6", 0, 6), v("IT6", 0, 6), v("TR6", 0, 6), OP.subtract)
+        tt(v("VM"), v("P7", 0, 96), v("MASK", 0, 96), OP.mult)
+        scan(v("ZV"), v("KEEP", 0, 96), v("VM"), OP.mult, OP.add)
+        cp("V", v("U6", 0, 6), v("ZV", 15, 96, 16))
+        ts(v("U6", 0, 6), v("U6", 0, 6), W - 1, AND)
+        ts(v("H6", 0, 6), v("U6", 0, 6), 5, SHR)
+        cp("V", v("UF", 0, 6), v("U6", 0, 6))
+        ts(v("H6", 0, 6), v("H6", 0, 6), 1.0, OP.add)
+        ts(v("UF2", 0, 6), v("U6", 0, 6), 2.0, OP.mult)
+        tt(v("T0F", 0, 6), v("U6", 0, 6), v("H6", 0, 6), OP.mult)
+        for c in range(6):
+            ts(v("TI", 32 * (c // 2) + c % 2, 32 * (c // 2) + 32, 2), v("M2", 0, 16), v("UF", c, c + 1), OP.mult, v("T0F", c, c + 1), OP.add)
+        ts(v("TI"), v("TI"), W - 1, AND)
+        cp("V", v("TL"), v("TI"))
+        ky = "P12"
+        mm(v(ky, 0, 96), v("IDN"), v("MK"), True, False)
+        for d in range(3):
+            o = v("AD", 512 * d, 512 * d + 512)
+            tt(o, ind(v("XR%d%d" % (rd, d)), v("TL", 32 * d, 32 * d + 32)), v("AR", 512 * d, 512 * d + 512), OP.subtract)
+            act(o, o, AF.Abs)
+        for a in range(16):
+            mm(v(ky, 0, 96), ez("EX", a), v("AD", a, 1536, 16), False, a == 15)
+        for c in range(6):
+            o, i_ = v("KM", c, c + 1), v(ky, 32 * (c // 2) + c % 2, 32 * (c // 2) + 32, 2)
+            emit("V", [i_], [o], lambda e, o=o, i_=i_: e.tensor_reduce(ap(o), ap(i_), AxisListType.X, OP.min))
+        for d in range(3):
+            ts(v("FD", 2 * d, 2 * d + 2), v("KM", 2 * d, 2 * d + 2), v("PR%d" % d, 1, 2), OP.is_lt)
+        cp("V", v("M6", 0, 6), v("KM", 0, 6))
+        tt(v("FD", 0, 6), v("FD", 0, 6), v("LV", 0, 6), OP.mult)
+        ts(v("M6", 0, 6), v("M6", 0, 6), 15, AND)
+        scan(v("FS", 0, 6), v("FD", 0, 6), v("FD", 0, 6), OP.add, OP.max)
+        cp("V", v("FB6", 0, 6), v("FD", 0, 6))
+        cp("V", v("CS", 1, 7), v("FS", 0, 6))
+        tt(v("CBF", 0, 6), v("M6", 0, 6), v("UF2", 0, 6), OP.mult)
+        mm(v("P7", 0, 6), v("LT4"), v("FB6", 0, 6), True, False)
+        mm(v("P7", 0, 6), v("BB4"), v("CS", 0, 6), False, True)
+        tt(v("CB", 0, 6), v("CBF", 0, 6), v("T0F", 0, 6), OP.add)
+        tt(v("P1", 0, 6), v("P7", 0, 6), v("IT6", 0, 6), OP.add)
+        ts(v("CB", 0, 6), v("CB", 0, 6), W - 1, AND)
+        tt(v("P1", 0, 6), v("P1", 0, 6), v("FD", 0, 6), OP.mult)
+        cp("V", v("CBF", 0, 6), v("CB", 0, 6))
+        tt(v("P1", 0, 6), v("P1", 0, 6), v("TR6", 0, 6), OP.add)
+        cp("V", v("PI6", 0, 6), v("P1", 0, 6))
+        ts(v("X6", 0, 6), v("PI6", 0, 6), 15, AND)
+        ts(v("SI6", 0, 6), v("PI6", 0, 6), 2, SHR)
+        cp("V", v("XF", 0, 6), v("X6", 0, 6))
+        cp("V", v("SL", 0, 6), v("SI6", 0, 6))
+        for c in range(6):
+            if c % 2:
+                act(v("EXB", 16 * c, 16 * c + 16), v("MASK", 0, 16), AF.Copy, scale=v("XF", c, c + 1))
+            else:
+                ts(v("EXB", 16 * c, 16 * c + 16), v("MASK", 0, 16), v("XF", c, c + 1), OP.mult)
+        mm(v("P0", 0, 96), v("BB"), v("EXB"))
+        for c in range(6):
+            o = 8 * (c // 2) + c % 2, 8 * (c // 2) + 8, 2
+            act(v("FIF", *o), v("F41", 0, 4), AF.Identity, bias=v("CBF", c, c + 1))
+        cp("V", v("FI", 0, 24), v("FIF", 0, 24))
+        ts(v("FI", 0, 24), v("FI", 0, 24), W - 1, AND)
+        cp("V", v("FL", 0, 24), v("FI", 0, 24))
+        for d in range(3):
+            cp("A", v("FB", 128 * d, 128 * d + 128), ind(v("XR%d%d" % (rd, d)), v("FL", 8 * d, 8 * d + 8)))
+        for c in range(6):
+            o = 8 * (c // 2) + c % 2, 8 * (c // 2) + 8, 2
+            act(v("FPF", *o), v("F4", 0, 4), AF.Identity, bias=v("P1", c, c + 1))
+        ts(v("KN"), v("P0", 0, 96), p15, OP.is_le, -4.0, OP.mult)
+        ts(v("CD"), v("P0", 0, 96), p15, OP.is_gt, -4.0, OP.mult)
+        cp("V", ind(v("WA", 0, 1304), v("SL", 0, 6)), v("KN"))
+        cp("V", ind(v("WB", 8, 1312), v("SL", 0, 6)), v("CD"))
+        for s in range(2):
+            o, h = (128 * s, 128 * s + 128), (512 * s, 512 * s + 512)
+            init = 0.0 if s == 0 else v("P34", 511, 512)
+            scan(v("P34", *h), v("WA", *h), v("WB", 512 * s + 4, 512 * s + 516), OP.add, OP.add, init)
+            tt(v("SR", *o), v("P34", 512 * s + 3, 512 * s + 512, 4), v("QF", *o), OP.add)
+            cp("V", v("SRL", *o), v("SR", *o))
+            cp("AV"[s], v(Xn, 2048 * s, 2048 * s + 2048), ind(v("Y0"), v("SRL", *o)))
+            if s == 0:
+                cp("V", v("FP", 0, 24), v("FPF", 0, 24))
+        cp("V", ind(v(Xn), v("FP", 0, 24)), v("FB"))
+    Xn = "XA" if RO % 2 == 0 else "XB"
+    for c in range(4):
+        x = v(Xn, 1024 * c, 1024 * c + 1024)
+        dma("SA"[c % 2], T.y[:, 1024 * c:1024 * c + 1024], ap(x), [x], [])
+    for s in SEMAPHORES:
+        if count.get(s, 0):
+            wait("G", s, count[s])

@@ -7,6 +7,11 @@ RO = 2
 XW = 5184
 F32, BF, I32, U16, F16 = "float32", "bfloat16", "int32", "uint16", "float16"
 SEGS = [(0, 192), (192, 256)]
+ON_SCALAR = ((1, 3),)
+TEN = ((0, 5), (5, 5))
+VEC = ((10, 3), (13, 3))
+WAKE = 0.06
+CY = 0.00083
 
 SCRATCH = {}
 PLACE = {}
@@ -35,10 +40,10 @@ _pack(768, I32, "kI", "CCX", "TM")
 _buf("sbuf", 768, U16, "CLX")
 _buf("sbuf", 256, F16, "NXH")
 _pack(128, I32, "gI", "J15", "JG", "J7")
-_pack(128, F32, "gF", "MASK", "KEEP", "KP8", "R0", "R1", "Z0", "Z1", "TT0", "TT1")
+_pack(128, F32, "gF", "MASK", "KEEP", "KP8", "R0", "R1", "Z0", "Z1", "Z2", "Z3", "TT0", "TT1")
 _pack(128, U16, "gU", "LE", "LO")
 _buf("sbuf", 640, F32, "RO0", "RO1")
-_buf("sbuf", 384, F32, "RO2", "ZOD", "MASK3", "KEEP3")
+_buf("sbuf", 384, F32, "ROV0", "ROV1", "ZOV0", "ZOV1", "MASK3", "KEEP3")
 _buf("sbuf", 512, F32, "IDV", "WTS")
 _buf("sbuf", 512, I32, "JI", "PB8")
 _buf("sbuf", 4608, F32, "SW")
@@ -84,7 +89,7 @@ def rank_program(g, core, T, topo):
     known = {q: {} for q in queue}
     snap = {}
     log = {}
-    ndma = [0]
+    ndma, now = [0], [0]
 
     def v(name, lo=0, hi=None, st=1):
         host, base, cols = PLACE[name]
@@ -111,6 +116,9 @@ def rank_program(g, core, T, topo):
         if a[2] == b[2] and a[2] > 1 and (a[0] - b[0]) % a[2]:
             return False
         return True
+
+    def inside(a, lo, hi, st):
+        return a[0] >= lo and a[1] <= hi and (st == 1 or (a[2] == st and (a[0] - lo) % st == 0))
 
     def bank(x):
         n, lo, hi, st = x
@@ -153,12 +161,14 @@ def rank_program(g, core, T, topo):
                 nm, lo, hi, st = bank(x)
                 l = log.setdefault(nm, [])
                 if wr:
-                    l[:] = [a for a in l if not (a[0] >= lo and a[1] <= hi and (st == 1 or (a[2] == st and (a[0] - lo) % st == 0)))]
+                    l[:] = [a for a in l if not inside(a, lo, hi, st)]
                 else:
                     l[:] = [a for a in l if not (a[3] == q and not a[4] and a[0] >= lo and a[1] <= hi and a[2] == st and st == 1)]
                 l.append((lo, hi, st, q, wr, sem, n))
 
-    def emit(q, reads, writes, fn):
+    ops = []
+
+    def record(q, reads, writes, cost, lag, issue):
         rd, wr = [], []
         for x in reads:
             if isinstance(x, tuple):
@@ -169,55 +179,152 @@ def rank_program(g, core, T, topo):
                 rd.append(x[2])
             else:
                 wr.append(x)
-        order(q, rd, wr)
-        s = qsem[q]
-        count[s] = count.get(s, 0) + 1
-        fn(queue[q]).then_inc(T.sem[s], 1)
-        snap[(s, count[s])] = dict(known[q])
-        note(q, rd, wr, s, count[s])
+        ops.append((q, rd, wr, cost, lag, issue))
+
+    def plan():
+        seen, preds, last = {}, [], {}
+        for i, (q, rd, wr, _, _, _) in enumerate(ops):
+            ps = set()
+            for lst, w in ((rd, False), (wr, True)):
+                for x in lst:
+                    n, lo, hi, st = bank(x)
+                    psum = SCRATCH[n][0] == "psum"
+                    for a in seen.get(n, ()):
+                        if hits((lo, hi, st), a) and (a[4] or w or (psum and ops[a[3]][0] != q)):
+                            ps.add(a[3])
+            if q in ("G", "S"):
+                if q in last:
+                    ps.add(last[q])
+                last[q] = i
+            for lst, w in ((rd, False), (wr, True)):
+                for x in lst:
+                    n, lo, hi, st = bank(x)
+                    l = seen.setdefault(n, [])
+                    if w:
+                        l[:] = [a for a in l if not inside(a, lo, hi, st)]
+                    l.append((lo, hi, st, i, w))
+            ps.discard(i)
+            preds.append(ps)
+        succ = [[] for _ in ops]
+        for i, ps in enumerate(preds):
+            for j in ps:
+                succ[j].append(i)
+
+        def between(i, j):
+            return 0.0 if ops[i][0] == ops[j][0] and ops[i][0] in ("P", "G", "S") else WAKE + ops[i][4]
+
+        prio = [0.0] * len(ops)
+        for i in range(len(ops) - 1, -1, -1):
+            prio[i] = ops[i][3] + max([prio[j] + between(i, j) for j in succ[i]], default=0.0)
+        left = [len(p) for p in preds]
+        at = [0.0] * len(ops)
+        free, ready, res = {}, {}, []
+        for i in range(len(ops)):
+            if not left[i]:
+                ready.setdefault(ops[i][0], []).append(i)
+        while ready:
+            best = None
+            for q, c in ready.items():
+                f = 0.0 if q is None else free.get(q, 0.0)
+                t0 = min(max(f, at[i]) for i in c)
+                if best is None or t0 < best[0]:
+                    best = (t0, q, f)
+            t0, q, f = best
+            c = ready[q]
+            i = max((i for i in c if max(f, at[i]) <= t0), key=lambda i: (prio[i], -i))
+            c.remove(i)
+            if not c:
+                del ready[q]
+            e = max(f, at[i]) + ops[i][3]
+            free[q] = e
+            res.append(i)
+            for j in succ[i]:
+                at[j] = max(at[j], e + between(i, j))
+                left[j] -= 1
+                if not left[j]:
+                    ready.setdefault(ops[j][0], []).append(j)
+        return res
+
+    def many(x):
+        if x[0] == "ind":
+            return 16 * (x[2][2] - x[2][1])
+        return (x[2] - x[1] + x[3] - 1) // x[3]
+
+    def half(x):
+        return SCRATCH[(x[1] if x[0] == "ind" else x)[0]][2] in (BF, U16, F16)
+
+    def cost(q, kind, out, ins):
+        n = many(out)
+        if kind == "mm":
+            return 0.00071 * max(64, many(ins[1])) * (4 if SCRATCH[ins[0][0]][2] == F32 else 1)
+        if kind == "iota":
+            return 0.13 + 2 * n * CY
+        if out[0] == "ind":
+            return 0.05 + 3.5 * n * CY
+        if any(x[0] == "ind" for x in ins):
+            return 0.05 + 1.5 * n * CY
+        if kind == "tt" and not any(SCRATCH[x[0]][0] == "psum" for x in ins):
+            n = 2 * n
+        if kind == "ts" and all(half(x) for x in ins + [out]):
+            n = n / 2
+        return max(n, 64) * CY + (0.05 if q == "A" else 0.03)
+
+    def emit(q, kind, reads, writes, fn):
+        def issue():
+            rd, wr = ops[now[0]][1:3]
+            order(q, rd, wr)
+            s = qsem[q]
+            count[s] = count.get(s, 0) + 1
+            fn(queue[q]).then_inc(T.sem[s], 1)
+            snap[(s, count[s])] = dict(known[q])
+            note(q, rd, wr, s, count[s])
+        record(q, reads, writes, cost(q, kind, writes[0], [x for x in reads if isinstance(x, tuple)]), 0.0, issue)
 
     def dma(q, out, in_, reads, writes):
-        order(q, reads, writes)
         s = "d%d" % ndma[0]
         ndma[0] += 1
-        count[s] = 16
-        queue[q].dma_start(out, in_).then_inc(T.sem[s], 16)
-        snap[(s, 16)] = dict(known[q])
-        note(q + "dma", reads, writes, s, 16)
+
+        def issue():
+            order(q, reads, writes)
+            count[s] = 16
+            queue[q].dma_start(out, in_).then_inc(T.sem[s], 16)
+            snap[(s, 16)] = dict(known[q])
+            note(q + "dma", reads, writes, s, 16)
+        record(q, reads, writes, 0.1, 3.5, issue)
 
     def tt(out, a, b, op):
-        emit("V", [a, b], [out], lambda e: e.tensor_tensor(opnd(out), opnd(a), opnd(b), op))
+        emit("V", "tt", [a, b], [out], lambda e: e.tensor_tensor(opnd(out), opnd(a), opnd(b), op))
 
     def ts(out, a, s1, op0, s2=None, op1=None):
         def f(e):
             if op1 is None:
                 return e.tensor_scalar(ap(out), opnd(a), arg(s1), None, op0)
             return e.tensor_scalar(ap(out), opnd(a), arg(s1), arg(s2), op0, op1)
-        emit("V", [a, s1, s2], [out], f)
+        emit("V", "ts", [a, s1, s2], [out], f)
 
     def cp(q, out, a):
         if q == "V":
-            emit("V", [a], [out], lambda e: e.tensor_copy(opnd(out), opnd(a)))
+            emit("V", "ts", [a], [out], lambda e: e.tensor_copy(opnd(out), opnd(a)))
         else:
-            emit("A", [a], [out], lambda e: e.activation(ap(out), opnd(a), AF.Copy))
+            emit("A", "", [a], [out], lambda e: e.activation(ap(out), opnd(a), AF.Copy))
 
     def act(out, a, func, bias=0.0, scale=1.0):
-        emit("A", [a, bias, scale], [out], lambda e: e.activation(ap(out), opnd(a), func, bias=arg(bias), scale=arg(scale)))
+        emit("A", "", [a, bias, scale], [out], lambda e: e.activation(ap(out), opnd(a), func, bias=arg(bias), scale=arg(scale)))
 
     def fill(out, c):
-        emit("V", [], [out], lambda e: e.memset(ap(out), c))
+        emit("V", "ts", [], [out], lambda e: e.memset(ap(out), c))
 
     def scan(out, a, b, op0, op1, init=0.0):
-        emit("V", [a, b, init], [out], lambda e: e.tensor_tensor_scan(ap(out), ap(a), ap(b), arg(init), op0, op1))
+        emit("V", "", [a, b, init], [out], lambda e: e.tensor_tensor_scan(ap(out), ap(a), ap(b), arg(init), op0, op1))
 
     def mm(out, l, r, start=True, stop=True):
-        emit("P", [l, r], [out], lambda e: e.matmul(ap(out), ap(l), ap(r), start, stop))
+        emit("P", "mm", [l, r], [out], lambda e: e.matmul(ap(out), ap(l), ap(r), start, stop))
 
     def iota(out, pattern, base, cm):
         if SCRATCH[out[0]][2] == I32:
-            emit("G", [], [out], lambda e: e.iota(ap(out), pattern, base, cm))
+            emit("G", "iota", [], [out], lambda e: e.iota(ap(out), pattern, base, cm))
         else:
-            emit("G", [], [out], lambda e: e.iota(ap(out), pattern, base, cm, allow_small_or_imprecise_dtypes=True))
+            emit("G", "iota", [], [out], lambda e: e.iota(ap(out), pattern, base, cm, allow_small_or_imprecise_dtypes=True))
 
     def ez(n, a):
         return v(n, 15 - a, 143 - a)
@@ -265,31 +372,30 @@ def rank_program(g, core, T, topo):
     for k in range(3):
         cp("A", v("MASK3", 128 * k, 128 * k + 128), v("MASK"))
         cp("A", v("KEEP3", 128 * k, 128 * k + 128), v("KEEP"))
-
-    def late_constants():
-        ts(v("K2", 0, 128), v("J7"), 0.0, OP.is_gt, 2.0, OP.mult)
-        ts(v("K2", 128, 256), v("J7"), 0.0, OP.is_gt, 2.0, OP.mult)
-        ts(v("BB4"), v("JG"), pg, OP.is_equal, 4.0, OP.mult)
-        ts(v("TT0"), J, pf, OP.is_gt)
-        ts(v("TT1"), J, pf, OP.is_lt)
-        tt(v("LT"), v("TT0"), v("BB"), OP.mult)
-        tt(v("UT"), v("TT1"), v("BB"), OP.mult)
-        ts(v("LT4"), v("LT"), 4.0, OP.mult)
-        ts(v("EX"), v("EZ"), 16.0, OP.mult)
-        ts(v("EZF"), v("EZ"), 0.0625, OP.mult)
-        ts(v("LE", 0, 8), v("QF", 0, 8), 32.0, OP.mult)
-        ts(v("WTS"), v("PB8"), 4096.0, OP.mult, float(1 << 21), OP.add)
-        ts(v("IDV"), v("JI"), 8.0, OP.mult)
-        tt(v("IDV"), v("IDV"), v("WTS"), OP.add)
-        ts(v("TRJ"), v("QF", 0, 32), 4096.0, OP.add)
-        ts(v("TR6", 0, 6), v("QF", 0, 6), 4.0, OP.mult, 4800.0, OP.add)
-        ts(v("M2", 0, 16), v("JI", 0, 16), 2.0, OP.mult)
-        cp("V", v("F4", 0, 4), v("JI", 0, 4))
-        ts(v("F41", 0, 4), v("JI", 0, 4), 1.0, OP.add)
-        ts(v("TI"), v("JI", 0, 96), 1, SHR, 15, AND)
-        cp("V", v("MK"), v("TI"))
-        fill(v("EB", 0, 4), 0.0)
-        fill(v("CS", 0, 1), 0.0)
+    ts(v("K2", 0, 128), v("J7"), 0.0, OP.is_gt, 2.0, OP.mult)
+    ts(v("K2", 128, 256), v("J7"), 0.0, OP.is_gt, 2.0, OP.mult)
+    ts(v("BB4"), v("JG"), pg, OP.is_equal, 4.0, OP.mult)
+    ts(v("TT0"), J, pf, OP.is_gt)
+    ts(v("TT1"), J, pf, OP.is_lt)
+    tt(v("LT"), v("TT0"), v("BB"), OP.mult)
+    tt(v("UT"), v("TT1"), v("BB"), OP.mult)
+    ts(v("LT4"), v("LT"), 4.0, OP.mult)
+    ts(v("EX"), v("EZ"), 16.0, OP.mult)
+    ts(v("EZF"), v("EZ"), 0.0625, OP.mult)
+    ts(v("LE", 0, 8), v("QF", 0, 8), 32.0, OP.mult)
+    ts(v("SB", 0, 256, 32), v("QF", 0, 8), 32.0, OP.mult, -2048.0, OP.add)
+    ts(v("WTS"), v("PB8"), 4096.0, OP.mult, float(1 << 21), OP.add)
+    ts(v("IDV"), v("JI"), 8.0, OP.mult)
+    tt(v("IDV"), v("IDV"), v("WTS"), OP.add)
+    ts(v("TRJ"), v("QF", 0, 32), 4096.0, OP.add)
+    ts(v("TR6", 0, 6), v("QF", 0, 6), 4.0, OP.mult, 4800.0, OP.add)
+    ts(v("M2", 0, 16), v("JI", 0, 16), 2.0, OP.mult)
+    cp("V", v("F4", 0, 4), v("JI", 0, 4))
+    ts(v("F41", 0, 4), v("JI", 0, 4), 1.0, OP.add)
+    ts(v("TI"), v("JI", 0, 96), 1, SHR, 15, AND)
+    cp("V", v("MK"), v("TI"))
+    fill(v("EB", 0, 4), 0.0)
+    fill(v("CS", 0, 1), 0.0)
 
     mine = topo.chip(core)
     mate = [c for c in cores if topo.mates(topo.chip(c), mine) and topo.die(c) == topo.die(core)][0]
@@ -307,17 +413,22 @@ def rank_program(g, core, T, topo):
         return DstId(rid=a[0], pnc=a[1])
 
     def remote(transfers, local, reads):
-        order("G", reads, [])
         n = sum(len(es) for _, _, _, es, _ in transfers)
-        count[local] = count.get(local, 0) + n
-        g.remote_dma_fused([RemoteDMATransfer(dst_ids=[dst(c)], dma_engine_mask=sum(1 << e for e in es), remote_sem=T.sem[rs], src=s, dst=d)
-                            for c, s, d, es, rs in transfers], local_sem=T.sem[local])
-        snap[(local, count[local])] = dict(known["G"])
-        note("Gremote", reads, [], local, count[local])
 
-    def arrives(name, lo, hi, sem, n):
-        count[sem] = n
-        note("remote", [], [v(name, lo, hi)], sem, n)
+        def issue():
+            order("G", reads, [])
+            count[local] = count.get(local, 0) + n
+            g.remote_dma_fused([RemoteDMATransfer(dst_ids=[dst(c)], dma_engine_mask=sum(1 << e for e in es), remote_sem=T.sem[rs], src=s, dst=d)
+                                for c, s, d, es, rs in transfers], local_sem=T.sem[local])
+            snap[(local, count[local])] = dict(known["G"])
+            note("Gremote", reads, [], local, count[local])
+        record("G", reads, [], 1.0, 8.0, issue)
+
+    def arrives(name, lo, hi, sem, n, like=()):
+        def issue():
+            count[sem] = n
+            note("remote", [], [v(name, lo, hi)], sem, n)
+        record(None, list(like), [v(name, lo, hi)], 0.0, 12.0, issue)
 
     for d in range(3):
         arrives("PR%d" % d, 0, 4, "par", 3)
@@ -335,10 +446,11 @@ def rank_program(g, core, T, topo):
             remote([(mate, ap(src), T["XR%d%d" % (rd, slot(mate, core))][:, lo:hi], off, "am%d%d" % (rd, h)),
                     (near, ap(src), T["XR%d%d" % (rd, slot(near, core))][:, lo:hi], on, "ap%d%d" % (rd, h))], "lx%d%d" % (rd, h), [src])
         for h, lo, hi in halves():
+            src = v(x, lo, hi)
             a, b, c = ("XR%d%d" % (rd, slot(core, o)) for o in (mate, near, diag))
-            arrives(a, lo, hi, "am%d%d" % (rd, h), len(off))
-            arrives(b, lo, hi, "ap%d%d" % (rd, h), len(on))
-            arrives(c, lo, hi, "aq%d%d" % (rd, h), len(on))
+            arrives(a, lo, hi, "am%d%d" % (rd, h), len(off), [src])
+            arrives(b, lo, hi, "ap%d%d" % (rd, h), len(on), [src])
+            arrives(c, lo, hi, "aq%d%d" % (rd, h), len(on), [src])
 
     def hand_on(rd):
         for h, lo, hi in halves():
@@ -362,8 +474,6 @@ def rank_program(g, core, T, topo):
         for s, (lo, hi) in enumerate(SEGS):
             for a in range(16):
                 mm(v(hb[s], 0, hi - lo), ez("EW", a), v(X, 16 * lo + a, 16 * hi, 16), a == 0, a == 15)
-        if rd == 0:
-            late_constants()
 
         def cl(m, lo, hi):
             if m == 3:
@@ -417,31 +527,25 @@ def rank_program(g, core, T, topo):
             for a in range(16):
                 mm((n, o, o + 64, 1), ez("EZ", a), v(buf, a, 1024, 16), a == 0, a == 15)
 
-        def vgather(m, q):
-            b = "DD%d" % (dn[0] % 4)
-            dn[0] += 1
-            tt(v(b), ind(v(X, 0, W), cl(m, 64 * q, 64 * q + 64)), v("Y0", 1024 * q, 1024 * q + 1024), OP.subtract)
-            return b
+        def unit(m, q):
+            win, x = ind(v(X, 0, W), cl(m, 64 * q, 64 * q + 64)), (1024 * q, 1024 * q + 1024)
+            if m == 3 or (m, q) in ON_SCALAR:
+                b, c = "GA%d" % (an[0] % 2), "AB%d" % (an[0] % 2)
+                an[0] += 1
+                for k in range(2):
+                    mm(v("P34", 512 * k, 512 * k + 512), v("NID"), v(X, x[0] + 512 * k, x[0] + 512 * k + 512), True, False)
+                cp("A", v(b), win)
+                for k in range(2):
+                    mm(v("P34", 512 * k, 512 * k + 512), v("IDN"), v(b, 512 * k, 512 * k + 512), False, True)
+                act(v(c), v("P34"), AF.Abs)
+            else:
+                c = "DD%d" % (dn[0] % 4)
+                dn[0] += 1
+                tt(v(c), win, v("Y0", *x), OP.subtract)
+                act(v(c), v(c), AF.Abs)
+            reduce_abs(m, q, c)
 
-        def aabs(m, q, b):
-            act(v(b), v(b), AF.Abs)
-            reduce_abs(m, q, b)
-
-        def agather(q):
-            b = "GA%d" % (an[0] % 2)
-            for k in range(2):
-                mm(v("P34", 512 * k, 512 * k + 512), v("NID"), v(X, 1024 * q + 512 * k, 1024 * q + 512 * k + 512), True, False)
-            cp("A", v(b), ind(v(X, 0, W), cl(3, 64 * q, 64 * q + 64)))
-            for k in range(2):
-                mm(v("P34", 512 * k, 512 * k + 512), v("IDN"), v(b, 512 * k, 512 * k + 512), False, True)
-
-        def aabs3(q):
-            b = "AB%d" % (an[0] % 2)
-            an[0] += 1
-            act(v(b), v("P34"), AF.Abs)
-            reduce_abs(3, q, b)
-
-        def nearest(s, ms, first, last):
+        def nearest(s, ms):
             lo, hi = SEGS[s]
             w = hi - lo
             o = (lo, hi)
@@ -451,47 +555,30 @@ def rank_program(g, core, T, topo):
                 kn[0] += 1
                 ts(pen, dist(m, s), t1, OP.is_ge, 65536.0, OP.mult)
                 tt(key, pen, v("CN%d" % m, *o), OP.add)
-                tt(v("KI", *o) if last and m == ms[-1] else run, v("DEF", *o) if first and m == ms[0] else run, key, OP.min)
-            if last:
-                ts(v("NXI", *o), v("KI", *o), W - 1, AND)
-                ts(v("NXH", *o), v("NXI", *o), -2048.0, OP.add)
-                cp("V", v("NXL", *o), v("NXI", *o))
-                banks = [("P56", 0), ("P56", 512), ("P7", 0)]
-                per = 512 // w
-                for i in range(0, 16, per):
-                    bn, b0 = banks[i // per % 3]
-                    for j in range(per):
-                        mm(v(bn, b0 + w * j, b0 + w * j + w), sel(i + j), v("NXH", *o))
-                    for j in range(per):
-                        cp("VA"[i // per % 2], v("NX1", 16 * lo + i + j, 16 * hi, 16), v(bn, b0 + w * j, b0 + w * j + w))
+                tt(v("KI", *o) if m == ms[-1] else run, v("DEF", *o) if m == ms[0] else run, key, OP.min)
+            ts(v("NXI", *o), v("KI", *o), W - 1, AND)
+            ts(v("NXH", *o), v("NXI", *o), -2048.0, OP.add)
+            cp("V", v("NXL", *o), v("NXI", *o))
+            banks = [("P56", 0), ("P56", 512), ("P7", 0)]
+            per = 512 // w
+            for i in range(0, 16, per):
+                bn, b0 = banks[i // per % 3]
+                for j in range(per):
+                    mm(v(bn, b0 + w * j, b0 + w * j + w), sel(i + j), v("NXH", *o))
+                for j in range(per):
+                    cp("VA"[i // per % 2], v("NX1", 16 * lo + i + j, 16 * hi, 16), v(bn, b0 + w * j, b0 + w * j + w))
 
-        looks(0)
-        agather(0)
-        aabs(0, 0, vgather(0, 0))
-        aabs3(0)
-        agather(1)
-        keys(0)
-        aabs(0, 1, vgather(0, 1))
-        aabs3(1)
-        aabs(0, 2, vgather(0, 2))
-        looks(1)
-        keys(1)
-        agather(2)
-        aabs(1, 0, vgather(1, 0))
-        aabs3(2)
-        aabs(1, 1, vgather(1, 1))
-        aabs(1, 2, vgather(1, 2))
-        aabs(2, 0, vgather(2, 0))
-        aabs(2, 1, vgather(2, 1))
-        agather(3)
-        aabs(2, 2, vgather(2, 2))
-        aabs3(3)
-        nearest(0, (0, 1), True, False)
-        aabs(0, 3, vgather(0, 3))
-        nearest(0, (3, 2), False, True)
-        aabs(1, 3, vgather(1, 3))
-        aabs(2, 3, vgather(2, 3))
-        nearest(1, (3, 0, 1, 2), True, True)
+        for s in range(2):
+            looks(s)
+            keys(s)
+        for q in range(3):
+            for m in (3, 0, 1, 2):
+                unit(m, q)
+        for m in (3, 0, 1):
+            unit(m, 3)
+        nearest(0, (0, 1, 3, 2))
+        unit(2, 3)
+        nearest(1, (3, 0, 1, 2))
         cp("V", v("NX2", 0, 2048), ind(v("NX1"), v("NXL", 0, 128)))
         cp("A", v("NX2", 2048, 4096), ind(v("NX1"), v("NXL", 128, 256)))
 
@@ -502,47 +589,41 @@ def rank_program(g, core, T, topo):
         def sb_of(k):
             return v("SB", k, 256, 32)
 
-        def odd_by_tensor(j, pb, ro):
-            cp("A", v(ro), ind(v("NX1"), v("LE", 8 * j, 8 * j + 40)))
+        def odd_by_tensor(j, n, pb, ro):
+            cp("A", v(ro, 0, 128 * n), ind(v("NX1"), v("LE", 8 * j, 8 * j + 8 * n)))
             for a in range(16):
-                mm(v(pb, 0, 40), ez("EZF", a), v(ro, a, 640, 16), a == 0, a == 15)
-
-        def odd_done(j, pb):
-            ts(v("LO", 8 * j, 8 * j + 40), v(pb, 0, 40), 2048.0, OP.add)
-            for k in range(5):
+                mm(v(pb, 0, 8 * n), ez("EZF", a), v(ro, a, 128 * n, 16), a == 0, a == 15)
+            ts(v("LO", 8 * j, 8 * j + 8 * n), v(pb, 0, 8 * n), 2048.0, OP.add)
+            for k in range(n):
                 cp("A", sb_of(2 * (j + k) + 1), v(pb, 8 * k, 8 * k + 8))
 
-        def odd_by_vector(j):
-            tt(v("RO2"), ind(v("NX1"), v("LE", 8 * j, 8 * j + 24)), v("MASK3"), OP.mult)
-            scan(v("ZOD"), v("KEEP3"), v("RO2"), OP.mult, OP.add)
-            ts(v("LO", 8 * j, 8 * j + 24), v("ZOD", 15, 384, 16), 2048.0, OP.add)
-            for k in range(3):
-                cp("V", sb_of(2 * (j + k) + 1), v("ZOD", 128 * k + 15, 128 * k + 128, 16))
+        def odd_by_vector(j, n, ro, zo):
+            w = 128 * n
+            tt(v(ro, 0, w), ind(v("NX1"), v("LE", 8 * j, 8 * j + 8 * n)), v("MASK3", 0, w), OP.mult)
+            scan(v(zo, 0, w), v("KEEP3", 0, w), v(ro, 0, w), OP.mult, OP.add)
+            ts(v("LO", 8 * j, 8 * j + 8 * n), v(zo, 15, w, 16), 2048.0, OP.add)
+            for k in range(n):
+                cp("V", sb_of(2 * (j + k) + 1), v(zo, 128 * k + 15, 128 * k + 128, 16))
 
         for i in range(16):
             le = v("LE", 8 * i, 8 * i + 8)
             if i < 15:
-                r, z = v("R%d" % (i % 2)), "Z%d" % (i % 2)
+                r, z = v("R%d" % (i % 2)), "Z%d" % (i % 4)
                 tt(r, ind(v("NX2"), le), v("MASK"), OP.mult)
                 scan(v(z), v("KEEP"), r, OP.mult, OP.add)
                 ts(v("LE", 8 * i + 8, 8 * i + 16), v(z, 15, 128, 16), 2048.0, OP.add)
-            if i == 4:
-                odd_by_tensor(0, "P0", "RO0")
-            if i == 9:
-                odd_by_tensor(5, "P7", "RO1")
+                cp("A", sb_of(2 * i + 2), v(z, 15, 128, 16))
             y0(2 * i)
-            if i == 11:
-                odd_done(0, "P0")
-                for k in range(5):
-                    y0(2 * k + 1)
-            if i == 12:
-                odd_by_vector(10)
-        odd_done(5, "P7")
-        odd_by_vector(13)
-        for b in range(8):
-            ts(v("SB", 32 * b, 32 * b + 32, 2), v("LE", b, 128, 8), -2048.0, OP.add)
-        for k in range(5, 16):
-            y0(2 * k + 1)
+            for e in range(2):
+                for lst, fn in ((TEN, odd_by_tensor), (VEC, odd_by_vector)):
+                    j, n = lst[e]
+                    if i == j + n - 1:
+                        if fn is odd_by_tensor:
+                            fn(j, n, ("P0", "P7")[e], "RO%d" % e)
+                        else:
+                            fn(j, n, "ROV%d" % e, "ZOV%d" % e)
+                        for k in range(j, j + n):
+                            y0(2 * k + 1)
         tt(v("DI", 0, 255), v("SB", 1, 256), v("SB", 0, 255), OP.subtract)
         ts(v("DI", 0, 255), v("DI", 0, 255), W - 1, AND)
         ts(v("FF", 0, 255), v("DI", 0, 255), 1.0, OP.not_equal)
@@ -627,7 +708,7 @@ def rank_program(g, core, T, topo):
             mm(v(ky, 0, 96), ez("EX", a), v("AD", a, 1536, 16), False, a == 15)
         for c in range(6):
             o, i_ = v("KM", c, c + 1), v(ky, 32 * (c // 2) + c % 2, 32 * (c // 2) + 32, 2)
-            emit("V", [i_], [o], lambda e, o=o, i_=i_: e.tensor_reduce(ap(o), ap(i_), AxisListType.X, OP.min))
+            emit("V", "", [i_], [o], lambda e, o=o, i_=i_: e.tensor_reduce(ap(o), ap(i_), AxisListType.X, OP.min))
         for d in range(3):
             ts(v("FD", 2 * d, 2 * d + 2), v("KM", 2 * d, 2 * d + 2), v("PR%d" % d, 1, 2), OP.is_lt)
         cp("V", v("M6", 0, 6), v("KM", 0, 6))
@@ -678,13 +759,15 @@ def rank_program(g, core, T, topo):
             tt(v("SR", *o), v("P34", 512 * s + 3, 512 * s + 512, 4), v("QF", *o), OP.add)
             cp("V", v("SRL", *o), v("SR", *o))
             cp("AV"[s], v(Xn, 2048 * s, 2048 * s + 2048), ind(v("Y0"), v("SRL", *o)))
-            if s == 0:
-                cp("V", v("FP", 0, 24), v("FPF", 0, 24))
+        cp("V", v("FP", 0, 24), v("FPF", 0, 24))
         cp("V", ind(v(Xn), v("FP", 0, 24)), v("FB"))
     Xn = "XA" if RO % 2 == 0 else "XB"
     for c in range(4):
         x = v(Xn, 1024 * c, 1024 * c + 1024)
         dma("SA"[c % 2], T.y[:, 1024 * c:1024 * c + 1024], ap(x), [x], [])
+    for i in plan():
+        now[0] = i
+        ops[i][5]()
     for s in SEMAPHORES:
         if count.get(s, 0):
             wait("G", s, count[s])

import numpy as np
from concourse.bass import DstId, RemoteDMATransfer
from concourse.mybir import dt, AluOpType as OP, AxisListType, ActivationFunctionType as AF

W = 4096
RO = 2
XW = 5184
F32, BF, I32, U16, F16 = "float32", "bfloat16", "int32", "uint16", "float16"
SEGS = [(0, 192), (192, 256)]
ON_SCALAR = ((1, 3),)
TEN = ((0, 5), (5, 5))
VEC = ((10, 3), (13, 3))
WAKE = 0.06
CY = 0.00083

SCRATCH = {}
PLACE = {}


def _buf(where, cols, dtype, *names):
    for n in names:
        SCRATCH[n] = (where, [128, cols], dtype)
        PLACE[n] = (n, 0, cols)


def _pack(cols, dtype, host, *names):
    SCRATCH[host] = ("sbuf", [128, cols * len(names)], dtype)
    for i, n in enumerate(names):
        PLACE[n] = (host, cols * i, cols)


_buf("sbuf", XW, BF, "XA", "XB")
_buf("sbuf", W, BF, "Y0", "XR00", "XR01", "XR02", "XR10", "XR11", "XR12")
_buf("sbuf", W, F32, "NX1", "NX2")
_buf("sbuf", 1024, BF, "DD0", "DD1", "DD2", "DD3", "GA0", "GA1", "AB0", "AB1")
_pack(256, I32, "hI", "CC3", "QI", "DI", "KI", "NXI", "UI", "HI")
_pack(256, U16, "hU", "CL3", "NXL", "SRL")
_pack(256, F32, "hF", "CN0", "CN1", "CN2", "CN3", "QF", "DEF", "K2", "SB", "FF", "CU", "WD", "SR", "KEY0", "KEY1")
_pack(768, I32, "kI", "CCX", "TM")
_buf("sbuf", 768, U16, "CLX")
_buf("sbuf", 256, F16, "NXH")
_pack(128, I32, "gI", "J15", "JG", "J7")
_pack(128, F32, "gF", "MASK", "KEEP", "KP8", "R0", "R1", "Z0", "Z1", "Z2", "Z3", "TT0", "TT1")
_pack(128, U16, "gU", "LE", "LO")
_buf("sbuf", 640, F32, "RO0", "RO1")
_buf("sbuf", 384, F32, "ROV0", "ROV1", "ZOV0", "ZOV1", "MASK3", "KEEP3")
_buf("sbuf", 512, F32, "IDV", "WTS")
_buf("sbuf", 512, I32, "JI", "PB8")
_buf("sbuf", 4608, F32, "SW")
_buf("sbuf", 1312, F32, "WA", "WB")
_buf("sbuf", 144, BF, "EZ", "EW", "EX")
_buf("sbuf", 144, F32, "EZF")
_buf("sbuf", 128, BF, "BB", "IDN", "NID", "LT", "UT", "LT4", "BB4", "WB0", "WB1", "WB2")
_buf("sbuf", 2048, F16, "SEL")
_buf("sbuf", 16, I32, "TH", "IC")
_buf("sbuf", 16, F32, "FC")
_buf("sbuf", 16, BF, "WT")
_buf("sbuf", 4, F32, "PAR", "PR0", "PR1", "PR2")
_pack(40, BF, "sB", "EB", "CX", "CS", "FB6")
_buf("sbuf", 32, F16, "W16")
_pack(32, F32, "sF", "TRJ", "ZE", "OF", "TR6", "M2", "F4", "F41", "T0F", "UF", "UF2", "I6", "IT6", "LV", "KM", "FD", "FS",
      "CBF", "P1", "XF", "Q6", "FIF", "FPF")
_pack(32, U16, "sU", "OL", "JL", "PL", "FL", "FP", "SL")
_pack(48, I32, "sI", "BI", "VI", "JX", "RX", "PX", "WI", "U6", "H6", "M6", "CB", "FI", "PI6", "SI6", "X6")
_pack(48, F32, "tF", "BF8", "CM8", "IN8")
_pack(96, F32, "uF", "KN", "CD", "RR", "VM", "ZV")
_pack(96, I32, "uI", "TI")
_pack(96, U16, "uU", "TL")
_pack(96, BF, "uB", "AQ", "MK", "EXB")
_buf("sbuf", 1536, BF, "AR", "AD")
_buf("sbuf", 384, BF, "FB")
_buf("psum", 512, F32, "P0", "P7")
_buf("psum", 1024, F32, "P12", "P34", "P56")

NDMA = 20
SEMAPHORES = ["sV", "sA", "sT", "sG", "par", "lpar"] + ["d%d" % i for i in range(NDMA)]
SEMAPHORES += ["%s%d%d" % (k, r, h) for k in ("am", "ap", "aq", "lx", "lf") for r in range(RO) for h in range(2)]


def rank_program(g, core, T, topo):
    rank = T.rank_of(core)
    if rank is None:
        return
    cores = list(T.cores)
    N = len(cores)
    queue = {"V": g.vector, "A": g.scalar, "P": g.tensor, "G": g, "S": g.sync}
    qsem = {"V": "sV", "A": "sA", "P": "sT", "G": "sG"}
    count = {}
    known = {q: {} for q in queue}
    snap = {}
    log = {}
    ndma, now = [0], [0]

    def v(name, lo=0, hi=None, st=1):
        host, base, cols = PLACE[name]
        return (host, base + lo, base + (cols if hi is None else hi), st)

    def ap(x):
        n, lo, hi, st = x
        return T[n][:, lo:hi] if st == 1 else T[n][:, lo:hi:st]

    def arg(x):
        return ap(x) if isinstance(x, tuple) else x

    def ind(win, off):
        return ("ind", win, off)

    def opnd(x):
        if x[0] == "ind":
            return ap(x[1]).indirect(ap(x[2]))
        return ap(x)

    def hits(a, b):
        if a[1] <= b[0] or b[1] <= a[0]:
            return False
        if a[2] == b[2] and a[2] > 1 and (a[0] - b[0]) % a[2]:
            return False
        return True

    def inside(a, lo, hi, st):
        return a[0] >= lo and a[1] <= hi and (st == 1 or (a[2] == st and (a[0] - lo) % st == 0))

    def bank(x):
        n, lo, hi, st = x
        if SCRATCH[n][0] == "psum":
            return n, lo // 512 * 512, (hi + 511) // 512 * 512, 1
        return x

    def wait(q, sem, n):
        if known[q].get(sem, 0) >= n:
            return
        queue[q].wait_ge(T.sem[sem], n)
        known[q][sem] = n
        for k, c in snap.get((sem, n), {}).items():
            if known[q].get(k, 0) < c:
                known[q][k] = c

    def order(q, reads, writes):
        need = {}
        for lst, wr in ((reads, False), (writes, True)):
            for x in lst:
                n, lo, hi, st = bank(x)
                ps = SCRATCH[n][0] == "psum"
                for a in log.get(n, ()):
                    aq, aw = a[3], a[4]
                    if not hits((lo, hi, st), a):
                        continue
                    if aq == q and q in qsem:
                        if not (aw or wr) or (ps and q == "P"):
                            continue
                    elif not (aw or wr or ps):
                        continue
                    if need.get(a[5], 0) < a[6]:
                        need[a[5]] = a[6]
        for sem in sorted(need, key=lambda s: -need[s]):
            wait(q, sem, need[sem])

    def note(q, reads, writes, sem, n):
        for lst, wr in ((reads, False), (writes, True)):
            for x in lst:
                nm, lo, hi, st = bank(x)
                l = log.setdefault(nm, [])
                if wr:
                    l[:] = [a for a in l if not inside(a, lo, hi, st)]
                else:
                    l[:] = [a for a in l if not (a[3] == q and not a[4] and a[0] >= lo and a[1] <= hi and a[2] == st and st == 1)]
                l.append((lo, hi, st, q, wr, sem, n))

    ops = []

    def record(q, reads, writes, cost, lag, issue):
        rd, wr = [], []
        for x in reads:
            if isinstance(x, tuple):
                rd += [x[1], x[2]] if x[0] == "ind" else [x]
        for x in writes:
            if x[0] == "ind":
                wr.append(x[1])
                rd.append(x[2])
            else:
                wr.append(x)
        ops.append((q, rd, wr, cost, lag, issue))

    def plan():
        seen, preds, last = {}, [], {}
        for i, (q, rd, wr, _, _, _) in enumerate(ops):
            ps = set()
            for lst, w in ((rd, False), (wr, True)):
                for x in lst:
                    n, lo, hi, st = bank(x)
                    psum = SCRATCH[n][0] == "psum"
                    for a in seen.get(n, ()):
                        if hits((lo, hi, st), a) and (a[4] or w or (psum and ops[a[3]][0] != q)):
                            ps.add(a[3])
            if q in ("G", "S"):
                if q in last:
                    ps.add(last[q])
                last[q] = i
            for lst, w in ((rd, False), (wr, True)):
                for x in lst:
                    n, lo, hi, st = bank(x)
                    l = seen.setdefault(n, [])
                    if w:
                        l[:] = [a for a in l if not inside(a, lo, hi, st)]
                    l.append((lo, hi, st, i, w))
            ps.discard(i)
            preds.append(ps)
        succ = [[] for _ in ops]
        for i, ps in enumerate(preds):
            for j in ps:
                succ[j].append(i)

        def between(i, j):
            return 0.0 if ops[i][0] == ops[j][0] and ops[i][0] in ("P", "G", "S") else WAKE + ops[i][4]

        prio = [0.0] * len(ops)
        for i in range(len(ops) - 1, -1, -1):
            prio[i] = ops[i][3] + max([prio[j] + between(i, j) for j in succ[i]], default=0.0)
        left = [len(p) for p in preds]
        at = [0.0] * len(ops)
        free, ready, res = {}, {}, []
        for i in range(len(ops)):
            if not left[i]:
                ready.setdefault(ops[i][0], []).append(i)
        while ready:
            best = None
            for q, c in ready.items():
                f = 0.0 if q is None else free.get(q, 0.0)
                t0 = min(max(f, at[i]) for i in c)
                if best is None or t0 < best[0]:
                    best = (t0, q, f)
            t0, q, f = best
            c = ready[q]
            i = max((i for i in c if max(f, at[i]) <= t0), key=lambda i: (prio[i], -i))
            c.remove(i)
            if not c:
                del ready[q]
            e = max(f, at[i]) + ops[i][3]
            free[q] = e
            res.append(i)
            for j in succ[i]:
                at[j] = max(at[j], e + between(i, j))
                left[j] -= 1
                if not left[j]:
                    ready.setdefault(ops[j][0], []).append(j)
        return res

    def many(x):
        if x[0] == "ind":
            return 16 * (x[2][2] - x[2][1])
        return (x[2] - x[1] + x[3] - 1) // x[3]

    def half(x):
        return SCRATCH[(x[1] if x[0] == "ind" else x)[0]][2] in (BF, U16, F16)

    def cost(q, kind, out, ins):
        n = many(out)
        if kind == "mm":
            return 0.00071 * max(64, many(ins[1])) * (4 if SCRATCH[ins[0][0]][2] == F32 else 1)
        if kind == "iota":
            return 0.13 + 2 * n * CY
        if out[0] == "ind":
            return 0.05 + 3.5 * n * CY
        if any(x[0] == "ind" for x in ins):
            return 0.05 + 1.5 * n * CY
        if kind == "tt" and not any(SCRATCH[x[0]][0] == "psum" for x in ins):
            n = 2 * n
        if kind == "ts" and all(half(x) for x in ins + [out]):
            n = n / 2
        return max(n, 64) * CY + (0.05 if q == "A" else 0.03)

    def emit(q, kind, reads, writes, fn):
        def issue():
            rd, wr = ops[now[0]][1:3]
            order(q, rd, wr)
            s = qsem[q]
            count[s] = count.get(s, 0) + 1
            fn(queue[q]).then_inc(T.sem[s], 1)
            snap[(s, count[s])] = dict(known[q])
            note(q, rd, wr, s, count[s])
        record(q, reads, writes, cost(q, kind, writes[0], [x for x in reads if isinstance(x, tuple)]), 0.0, issue)

    def dma(q, out, in_, reads, writes):
        s = "d%d" % ndma[0]
        ndma[0] += 1

        def issue():
            order(q, reads, writes)
            count[s] = 16
            queue[q].dma_start(out, in_).then_inc(T.sem[s], 16)
            snap[(s, 16)] = dict(known[q])
            note(q + "dma", reads, writes, s, 16)
        record(q, reads, writes, 0.1, 3.5, issue)

    def tt(out, a, b, op):
        emit("V", "tt", [a, b], [out], lambda e: e.tensor_tensor(opnd(out), opnd(a), opnd(b), op))

    def ts(out, a, s1, op0, s2=None, op1=None):
        def f(e):
            if op1 is None:
                return e.tensor_scalar(ap(out), opnd(a), arg(s1), None, op0)
            return e.tensor_scalar(ap(out), opnd(a), arg(s1), arg(s2), op0, op1)
        emit("V", "ts", [a, s1, s2], [out], f)

    def cp(q, out, a):
        if q == "V":
            emit("V", "ts", [a], [out], lambda e: e.tensor_copy(opnd(out), opnd(a)))
        else:
            emit("A", "", [a], [out], lambda e: e.activation(ap(out), opnd(a), AF.Copy))

    def act(out, a, func, bias=0.0, scale=1.0):
        emit("A", "", [a, bias, scale], [out], lambda e: e.activation(ap(out), opnd(a), func, bias=arg(bias), scale=arg(scale)))

    def fill(out, c):
        emit("V", "ts", [], [out], lambda e: e.memset(ap(out), c))

    def scan(out, a, b, op0, op1, init=0.0):
        emit("V", "", [a, b, init], [out], lambda e: e.tensor_tensor_scan(ap(out), ap(a), ap(b), arg(init), op0, op1))

    def mm(out, l, r, start=True, stop=True):
        emit("P", "mm", [l, r], [out], lambda e: e.matmul(ap(out), ap(l), ap(r), start, stop))

    def iota(out, pattern, base, cm):
        if SCRATCH[out[0]][2] == I32:
            emit("G", "iota", [], [out], lambda e: e.iota(ap(out), pattern, base, cm))
        else:
            emit("G", "iota", [], [out], lambda e: e.iota(ap(out), pattern, base, cm, allow_small_or_imprecise_dtypes=True))

    def ez(n, a):
        return v(n, 15 - a, 143 - a)

    def sel(a):
        return v("SEL", 128 * a, 128 * a + 128)

    AND, SHR = OP.bitwise_and, OP.logical_shift_right
    wtq = v("WT", 0, 1)
    dma("S", ap(wtq), T.wt[:], [], [wtq])
    dma("A", ap(v("TH", 0, 2)), T.th[:], [], [v("TH", 0, 2)])
    for n in ("XA", "Y0"):
        for c in range(4):
            x = v(n, 1024 * c, 1024 * c + 1024)
            dma("SA"[c % 2], ap(x), T.x0[:, 1024 * c:1024 * c + 1024], [], [x])
    iota(v("IC", 0, 1), [[1, 1]], 0, 1)
    iota(v("JI"), [[1, 512]], 0, 0)
    iota(v("QI"), [[16, 256]], 0, 1)
    iota(v("PB8"), [[64, 8], [1, 4], [4, 16]], 0, 0)
    ts(v("IC", 1, 2), v("IC", 0, 1), 15, AND)
    ts(v("IC", 2, 3), v("IC", 0, 1), 112, AND)
    fill(v("EZ"), 0.0)
    fill(v("PAR", 2, 4), 0.0)
    cp("V", v("FC", 0, 3), v("IC", 0, 3))
    pf, p15, pg, t1 = v("FC", 0, 1), v("FC", 1, 2), v("FC", 2, 3), v("FC", 3, 4)
    J = v("JI", 0, 128)
    cp("V", v("PAR", 0, 1), wtq)
    ts(v("PAR", 1, 2), v("TH", 1, 2), 16.0, OP.mult)
    cp("V", t1, v("TH", 0, 1))
    ts(v("EZ", 15, 143), J, pg, OP.is_equal)
    ts(v("IDN"), J, pf, OP.is_equal)
    ts(v("EW"), v("EZ"), wtq, OP.mult)
    ts(v("NID"), J, pf, OP.is_equal, -1.0, OP.mult)
    ts(v("QF"), v("QI"), pg, OP.subtract)
    ts(v("J15"), J, 15, AND)
    ts(v("JG"), J, 112, AND)
    ts(v("J7"), J, 7, AND)
    ts(v("MASK"), v("J15"), p15, OP.is_equal)
    ts(v("BB"), v("JG"), pg, OP.is_equal)
    ts(v("KEEP"), v("J15"), 0.0, OP.not_equal)
    ts(v("KP8"), v("J7"), 0.0, OP.not_equal)
    for a in range(16):
        ts(sel(a), v("BB"), v("MASK", a, a + 1), OP.mult)
    ts(v("DEF"), v("QF"), 32769.0, OP.add)
    for k in range(3):
        cp("A", v("MASK3", 128 * k, 128 * k + 128), v("MASK"))
        cp("A", v("KEEP3", 128 * k, 128 * k + 128), v("KEEP"))
    ts(v("K2", 0, 128), v("J7"), 0.0, OP.is_gt, 2.0, OP.mult)
    ts(v("K2", 128, 256), v("J7"), 0.0, OP.is_gt, 2.0, OP.mult)
    ts(v("BB4"), v("JG"), pg, OP.is_equal, 4.0, OP.mult)
    ts(v("TT0"), J, pf, OP.is_gt)
    ts(v("TT1"), J, pf, OP.is_lt)
    tt(v("LT"), v("TT0"), v("BB"), OP.mult)
    tt(v("UT"), v("TT1"), v("BB"), OP.mult)
    ts(v("LT4"), v("LT"), 4.0, OP.mult)
    ts(v("EX"), v("EZ"), 16.0, OP.mult)
    ts(v("EZF"), v("EZ"), 0.0625, OP.mult)
    ts(v("LE", 0, 8), v("QF", 0, 8), 32.0, OP.mult)
    ts(v("SB", 0, 256, 32), v("QF", 0, 8), 32.0, OP.mult, -2048.0, OP.add)
    ts(v("WTS"), v("PB8"), 4096.0, OP.mult, float(1 << 21), OP.add)
    ts(v("IDV"), v("JI"), 8.0, OP.mult)
    tt(v("IDV"), v("IDV"), v("WTS"), OP.add)
    ts(v("TRJ"), v("QF", 0, 32), 4096.0, OP.add)
    ts(v("TR6", 0, 6), v("QF", 0, 6), 4.0, OP.mult, 4800.0, OP.add)
    ts(v("M2", 0, 16), v("JI", 0, 16), 2.0, OP.mult)
    cp("V", v("F4", 0, 4), v("JI", 0, 4))
    ts(v("F41", 0, 4), v("JI", 0, 4), 1.0, OP.add)
    ts(v("TI"), v("JI", 0, 96), 1, SHR, 15, AND)
    cp("V", v("MK"), v("TI"))
    fill(v("EB", 0, 4), 0.0)
    fill(v("CS", 0, 1), 0.0)

    mine = topo.chip(core)
    mate = [c for c in cores if topo.mates(topo.chip(c), mine) and topo.die(c) == topo.die(core)][0]
    near = [c for c in cores if c != core and topo.chip(c) == mine][0]
    diag = [c for c in cores if c not in (core, mate, near)][0]

    def slot(receiver, owner):
        return (T.rank_of(owner) - T.rank_of(receiver) - 1) % N

    off = topo.engines(core, mate)
    on = [e for e in topo.engines(core, near) if e not in off]

    def dst(c):
        a = topo.addr(c)
        return DstId(rid=a[0], pnc=a[1])

    def remote(transfers, local, reads):
        n = sum(len(es) for _, _, _, es, _ in transfers)

        def issue():
            order("G", reads, [])
            count[local] = count.get(local, 0) + n
            g.remote_dma_fused([RemoteDMATransfer(dst_ids=[dst(c)], dma_engine_mask=sum(1 << e for e in es), remote_sem=T.sem[rs], src=s, dst=d)
                                for c, s, d, es, rs in transfers], local_sem=T.sem[local])
            snap[(local, count[local])] = dict(known["G"])
            note("Gremote", reads, [], local, count[local])
        record("G", reads, [], 1.0, 8.0, issue)

    def arrives(name, lo, hi, sem, n, like=()):
        def issue():
            count[sem] = n
            note("remote", [], [v(name, lo, hi)], sem, n)
        record(None, list(like), [v(name, lo, hi)], 0.0, 12.0, issue)

    for d in range(3):
        arrives("PR%d" % d, 0, 4, "par", 3)

    def send_params():
        remote([(c, ap(v("PAR")), T["PR%d" % slot(c, core)][:], [es], "par")
                for c, es in ((near, on[0]), (mate, off[0]), (diag, off[1]))], "lpar", [v("PAR")])

    def halves():
        return [(h, 2048 * h, 2048 * h + 2048) for h in range(2)]

    def broadcast(rd, x):
        for h, lo, hi in halves():
            src = v(x, lo, hi)
            remote([(mate, ap(src), T["XR%d%d" % (rd, slot(mate, core))][:, lo:hi], off, "am%d%d" % (rd, h)),
                    (near, ap(src), T["XR%d%d" % (rd, slot(near, core))][:, lo:hi], on, "ap%d%d" % (rd, h))], "lx%d%d" % (rd, h), [src])
        for h, lo, hi in halves():
            src = v(x, lo, hi)
            a, b, c = ("XR%d%d" % (rd, slot(core, o)) for o in (mate, near, diag))
            arrives(a, lo, hi, "am%d%d" % (rd, h), len(off), [src])
            arrives(b, lo, hi, "ap%d%d" % (rd, h), len(on), [src])
            arrives(c, lo, hi, "aq%d%d" % (rd, h), len(on), [src])

    def hand_on(rd):
        for h, lo, hi in halves():
            src = v("XR%d%d" % (rd, slot(core, mate)), lo, hi)
            remote([(near, ap(src), T["XR%d%d" % (rd, slot(near, mate))][:, lo:hi], on, "aq%d%d" % (rd, h))], "lf%d%d" % (rd, h), [src])

    for rd in range(RO):
        X, Xn = ("XA", "XB") if rd % 2 == 0 else ("XB", "XA")
        if rd > 0:
            for c in range(4):
                x, y = v(X, 1024 * c, 1024 * c + 1024), v("Y0", 1024 * c, 1024 * c + 1024)
                dma("S", ap(y), ap(x), [x], [y])
        broadcast(rd, X)
        if rd == 0:
            send_params()
        iota(v("SW", 0, 96), [[0, 96]], 0, 0)
        iota(v("WA", 0, 1024), [[0, 1024]], 0, 0)
        iota(v("WB", 4, 1032), [[0, 1028]], 0, 0)
        hand_on(rd)
        hb = ["P0", "P7"]
        for s, (lo, hi) in enumerate(SEGS):
            for a in range(16):
                mm(v(hb[s], 0, hi - lo), ez("EW", a), v(X, 16 * lo + a, 16 * hi, 16), a == 0, a == 15)

        def cl(m, lo, hi):
            if m == 3:
                return v("CL3", lo, hi)
            s0, s1 = SEGS[0] if hi <= SEGS[0][1] else SEGS[1]
            o = 3 * s0 + m * (s1 - s0) - s0
            return v("CLX", o + lo, o + hi)

        def looks(s):
            lo, hi = SEGS[s]
            w = hi - lo
            u, hm, u2 = v("UI", 0, w), v(hb[s], w, 2 * w), v(hb[s], 0, w)
            t = [v("TM", m * w, m * w + w) for m in range(3)]
            cp("V", u, v(hb[s], 0, w))
            ts(u, u, W - 1, AND)
            ts(v("HI", 0, w), u, 5, SHR)
            ts(hm, v("HI", 0, w), 7.0, OP.add)
            tt(t[0], hm, u, OP.mult)
            ts(v("CC3", lo, hi), t[0], W - 1, AND)
            cp("V", v("CL3", lo, hi), v("CC3", lo, hi))
            ts(hm, v("HI", 0, w), 1.0, OP.add)
            tt(t[0], hm, u, OP.mult)
            ts(u2, u, 2.0, OP.mult)
            tt(t[1], u2, t[0], OP.add)
            tt(t[2], u2, t[1], OP.add)
            c = (3 * lo, 3 * hi)
            ts(v("CCX", *c), v("TM", 0, 3 * w), W - 1, AND)
            cp("V", v("CLX", *c), v("CCX", *c))

        def keys(s):
            lo, hi = SEGS[s]
            w = hi - lo
            for m in range(3):
                ts(v("CN%d" % m, lo, hi), v("CCX", 3 * lo + m * w, 3 * lo + m * w + w), float(1 + 8192 * m), OP.add)
            ts(v("CN3", lo, hi), v("CC3", lo, hi), float(1 + 8192 * 3), OP.add)

        dn, an, kn = [0], [0], [0]

        def dist(m, s):
            lo, hi = SEGS[s]
            w = hi - lo
            if s == 0:
                o = 512 * (m // 2) + w * (m % 2)
                return v("P12", o, o + w)
            return v("P34", 0, w) if m == 2 else v("P0", 64 * (m % 3) + 128 * (m // 3), 64 * (m % 3) + 128 * (m // 3) + w)

        def reduce_abs(m, q, buf):
            s = 0 if 64 * q + 64 <= SEGS[0][1] else 1
            n, o, _, _ = dist(m, s)
            o += 64 * q - SEGS[s][0]
            for a in range(16):
                mm((n, o, o + 64, 1), ez("EZ", a), v(buf, a, 1024, 16), a == 0, a == 15)

        def unit(m, q):
            win, x = ind(v(X, 0, W), cl(m, 64 * q, 64 * q + 64)), (1024 * q, 1024 * q + 1024)
            if m == 3 or (m, q) in ON_SCALAR:
                b, c = "GA%d" % (an[0] % 2), "AB%d" % (an[0] % 2)
                an[0] += 1
                for k in range(2):
                    mm(v("P34", 512 * k, 512 * k + 512), v("NID"), v(X, x[0] + 512 * k, x[0] + 512 * k + 512), True, False)
                cp("A", v(b), win)
                for k in range(2):
                    mm(v("P34", 512 * k, 512 * k + 512), v("IDN"), v(b, 512 * k, 512 * k + 512), False, True)
                act(v(c), v("P34"), AF.Abs)
            else:
                c = "DD%d" % (dn[0] % 4)
                dn[0] += 1
                tt(v(c), win, v("Y0", *x), OP.subtract)
                act(v(c), v(c), AF.Abs)
            reduce_abs(m, q, c)

        def nearest(s, ms):
            lo, hi = SEGS[s]
            w = hi - lo
            o = (lo, hi)
            pen, run = v("P56", 0, w), v("P56", 512, 512 + w)
            for m in ms:
                key = v("KEY%d" % (kn[0] % 2), 0, w)
                kn[0] += 1
                ts(pen, dist(m, s), t1, OP.is_ge, 65536.0, OP.mult)
                tt(key, pen, v("CN%d" % m, *o), OP.add)
                tt(v("KI", *o) if m == ms[-1] else run, v("DEF", *o) if m == ms[0] else run, key, OP.min)
            ts(v("NXI", *o), v("KI", *o), W - 1, AND)
            ts(v("NXH", *o), v("NXI", *o), -2048.0, OP.add)
            cp("V", v("NXL", *o), v("NXI", *o))
            banks = [("P56", 0), ("P56", 512), ("P7", 0)]
            per = 512 // w
            for i in range(0, 16, per):
                bn, b0 = banks[i // per % 3]
                for j in range(per):
                    mm(v(bn, b0 + w * j, b0 + w * j + w), sel(i + j), v("NXH", *o))
                for j in range(per):
                    cp("VA"[i // per % 2], v("NX1", 16 * lo + i + j, 16 * hi, 16), v(bn, b0 + w * j, b0 + w * j + w))

        for s in range(2):
            looks(s)
            keys(s)
        for q in range(3):
            for m in (3, 0, 1, 2):
                unit(m, q)
        for m in (3, 0, 1):
            unit(m, 3)
        nearest(0, (0, 1, 3, 2))
        unit(2, 3)
        nearest(1, (3, 0, 1, 2))
        cp("V", v("NX2", 0, 2048), ind(v("NX1"), v("NXL", 0, 128)))
        cp("A", v("NX2", 2048, 4096), ind(v("NX1"), v("NXL", 128, 256)))

        def y0(k):
            l = v("LE" if k % 2 == 0 else "LO", 8 * (k // 2), 8 * (k // 2) + 8)
            cp("A", v("Y0", k, W, 32), ind(v(X, 0, W), l))

        def sb_of(k):
            return v("SB", k, 256, 32)

        def odd_by_tensor(j, n, pb, ro):
            cp("A", v(ro, 0, 128 * n), ind(v("NX1"), v("LE", 8 * j, 8 * j + 8 * n)))
            for a in range(16):
                mm(v(pb, 0, 8 * n), ez("EZF", a), v(ro, a, 128 * n, 16), a == 0, a == 15)
            ts(v("LO", 8 * j, 8 * j + 8 * n), v(pb, 0, 8 * n), 2048.0, OP.add)
            for k in range(n):
                cp("A", sb_of(2 * (j + k) + 1), v(pb, 8 * k, 8 * k + 8))

        def odd_by_vector(j, n, ro, zo):
            w = 128 * n
            tt(v(ro, 0, w), ind(v("NX1"), v("LE", 8 * j, 8 * j + 8 * n)), v("MASK3", 0, w), OP.mult)
            scan(v(zo, 0, w), v("KEEP3", 0, w), v(ro, 0, w), OP.mult, OP.add)
            ts(v("LO", 8 * j, 8 * j + 8 * n), v(zo, 15, w, 16), 2048.0, OP.add)
            for k in range(n):
                cp("V", sb_of(2 * (j + k) + 1), v(zo, 128 * k + 15, 128 * k + 128, 16))

        for i in range(16):
            le = v("LE", 8 * i, 8 * i + 8)
            if i < 15:
                r, z = v("R%d" % (i % 2)), "Z%d" % (i % 4)
                tt(r, ind(v("NX2"), le), v("MASK"), OP.mult)
                scan(v(z), v("KEEP"), r, OP.mult, OP.add)
                ts(v("LE", 8 * i + 8, 8 * i + 16), v(z, 15, 128, 16), 2048.0, OP.add)
                cp("A", sb_of(2 * i + 2), v(z, 15, 128, 16))
            y0(2 * i)
            for e in range(2):
                for lst, fn in ((TEN, odd_by_tensor), (VEC, odd_by_vector)):
                    j, n = lst[e]
                    if i == j + n - 1:
                        if fn is odd_by_tensor:
                            fn(j, n, ("P0", "P7")[e], "RO%d" % e)
                        else:
                            fn(j, n, "ROV%d" % e, "ZOV%d" % e)
                        for k in range(j, j + n):
                            y0(2 * k + 1)
        tt(v("DI", 0, 255), v("SB", 1, 256), v("SB", 0, 255), OP.subtract)
        ts(v("DI", 0, 255), v("DI", 0, 255), W - 1, AND)
        ts(v("FF", 0, 255), v("DI", 0, 255), 1.0, OP.not_equal)
        fill(v("FF", 31, 256, 32), 0.0)
        scan(v("CU"), v("FF"), v("FF"), OP.add, OP.max)
        scan(v("WD"), v("K2"), v("FF"), OP.mult, OP.add)
        for k in range(4):
            cp("V", v("EB", 4 + k, 36, 4), v("CU", 31, 256, 32))
        tt(v("CX", 0, 32), v("CU", 0, 256, 8), v("FF", 0, 256, 8), OP.subtract)
        first = v("P12", 0, 32)
        mm(first, v("LT"), v("EB", 4, 36), True, False)
        mm(first, v("UT"), v("EB", 0, 32), False, False)
        mm(first, v("IDN"), v("CX", 0, 32), False, True)
        cp("V", v("W16"), v("WD", 7, 256, 8))
        for a in range(16):
            mm(v("P12", 512 + a, 1024, 16), sel(a), v("W16"))
        cp("A", v("WTS"), v("P12", 512, 1024))
        mm(v("P0", 0, 1), v("BB"), v("EB", 35, 36))
        ts(v("ZE"), v("WD", 7, 256, 8), 0.0, OP.is_equal)
        tt(v("ZE"), v("ZE"), v("TRJ"), OP.mult)
        tt(v("OF"), first, v("ZE"), OP.max)
        cp("V", v("OL"), v("OF"))
        cp("V", ind(v("SW"), v("OL")), v("IDV"))
        ts(v("KN"), v("SW", 0, 96), 0.0, OP.is_equal)
        scan(v("CD"), v("KN"), v("SW", 0, 96), OP.mult, OP.add)
        scan(v("RR"), v("KN"), v("KN"), OP.mult, OP.add)
        tt(v("VM"), v("CD"), v("RR"), OP.add)
        tt(v("VM"), v("VM"), v("MASK", 0, 96), OP.mult)
        scan(v("ZV"), v("KEEP", 0, 96), v("VM"), OP.mult, OP.add)
        cp("V", v("VI", 0, 6), v("ZV", 15, 96, 16))
        ts(v("JX", 0, 6), v("VI", 0, 6), 3, SHR, 511, AND)
        ts(v("RX", 0, 6), v("VI", 0, 6), 7, AND)
        cp("V", v("JL", 0, 6), v("JX", 0, 6))
        ts(v("PX", 0, 6), v("VI", 0, 6), 12, SHR, 511, AND)
        tt(v("VM"), ind(v("WTS"), v("JL", 0, 6)), v("MASK", 0, 96), OP.mult)
        ts(v("Q6", 0, 6), v("PX", 0, 6), 8.0, OP.mult)
        scan(v("ZV"), v("KEEP", 0, 96), v("VM"), OP.mult, OP.add)
        ts(v("LV", 0, 6), v("QF", 0, 6), v("P0", 0, 1), OP.is_lt)
        cp("V", v("WI", 0, 6), v("ZV", 15, 96, 16))
        for k in range(8):
            ts(v("BI", k, 48, 8), v("WI", 0, 6), 7 - k, SHR, 1, AND)
        cp("V", v("BF8"), v("BI"))
        tt(v("BF8", 0, 48, 8), v("BI", 0, 48, 8), v("RX", 0, 6), OP.subtract)
        scan(v("CM8"), v("KP8", 0, 48), v("BF8"), OP.mult, OP.add)
        ts(v("IN8"), v("CM8"), 0.0, OP.is_le)
        scan(v("CM8"), v("KP8", 0, 48), v("IN8"), OP.mult, OP.add)
        tt(v("I6", 0, 6), v("Q6", 0, 6), v("CM8", 7, 48, 8), OP.add)
        ts(v("PL", 0, 6), v("I6", 0, 6), 4095.0, OP.min)
        cp("V", v("AQ"), ind(v("Y0"), v("PL", 0, 6)))
        if rd == 0:
            for d in range(3):
                ts(v("WB%d" % d), v("BB"), v("PR%d" % d, 0, 1), OP.mult)
        for d in range(3):
            mm(v("P7", 32 * d, 32 * d + 32), v("WB%d" % d), v("AQ", 32 * d, 32 * d + 32))
        for d in range(3):
            o = 512 * d
            cp("A", v("AR", o, o + 32), v("AQ", 32 * d, 32 * d + 32))
            for w in (32, 64, 128, 256):
                cp("A", v("AR", o + w, o + 2 * w), v("AR", o, o + w))
        ts(v("IT6", 0, 6), v("I6", 0, 6), 1.0, OP.add)
        tt(v("IT6", 0, 6), v("IT6", 0, 6), v("TR6", 0, 6), OP.subtract)
        tt(v("VM"), v("P7", 0, 96), v("MASK", 0, 96), OP.mult)
        scan(v("ZV"), v("KEEP", 0, 96), v("VM"), OP.mult, OP.add)
        cp("V", v("U6", 0, 6), v("ZV", 15, 96, 16))
        ts(v("U6", 0, 6), v("U6", 0, 6), W - 1, AND)
        ts(v("H6", 0, 6), v("U6", 0, 6), 5, SHR)
        cp("V", v("UF", 0, 6), v("U6", 0, 6))
        ts(v("H6", 0, 6), v("H6", 0, 6), 1.0, OP.add)
        ts(v("UF2", 0, 6), v("U6", 0, 6), 2.0, OP.mult)
        tt(v("T0F", 0, 6), v("U6", 0, 6), v("H6", 0, 6), OP.mult)
        for c in range(6):
            ts(v("TI", 32 * (c // 2) + c % 2, 32 * (c // 2) + 32, 2), v("M2", 0, 16), v("UF", c, c + 1), OP.mult, v("T0F", c, c + 1), OP.add)
        ts(v("TI"), v("TI"), W - 1, AND)
        cp("V", v("TL"), v("TI"))
        ky = "P12"
        mm(v(ky, 0, 96), v("IDN"), v("MK"), True, False)
        for d in range(3):
            o = v("AD", 512 * d, 512 * d + 512)
            tt(o, ind(v("XR%d%d" % (rd, d)), v("TL", 32 * d, 32 * d + 32)), v("AR", 512 * d, 512 * d + 512), OP.subtract)
            act(o, o, AF.Abs)
        for a in range(16):
            mm(v(ky, 0, 96), ez("EX", a), v("AD", a, 1536, 16), False, a == 15)
        for c in range(6):
            o, i_ = v("KM", c, c + 1), v(ky, 32 * (c // 2) + c % 2, 32 * (c // 2) + 32, 2)
            emit("V", "", [i_], [o], lambda e, o=o, i_=i_: e.tensor_reduce(ap(o), ap(i_), AxisListType.X, OP.min))
        for d in range(3):
            ts(v("FD", 2 * d, 2 * d + 2), v("KM", 2 * d, 2 * d + 2), v("PR%d" % d, 1, 2), OP.is_lt)
        cp("V", v("M6", 0, 6), v("KM", 0, 6))
        tt(v("FD", 0, 6), v("FD", 0, 6), v("LV", 0, 6), OP.mult)
        ts(v("M6", 0, 6), v("M6", 0, 6), 15, AND)
        scan(v("FS", 0, 6), v("FD", 0, 6), v("FD", 0, 6), OP.add, OP.max)
        cp("V", v("FB6", 0, 6), v("FD", 0, 6))
        cp("V", v("CS", 1, 7), v("FS", 0, 6))
        tt(v("CBF", 0, 6), v("M6", 0, 6), v("UF2", 0, 6), OP.mult)
        mm(v("P7", 0, 6), v("LT4"), v("FB6", 0, 6), True, False)
        mm(v("P7", 0, 6), v("BB4"), v("CS", 0, 6), False, True)
        tt(v("CB", 0, 6), v("CBF", 0, 6), v("T0F", 0, 6), OP.add)
        tt(v("P1", 0, 6), v("P7", 0, 6), v("IT6", 0, 6), OP.add)
        ts(v("CB", 0, 6), v("CB", 0, 6), W - 1, AND)
        tt(v("P1", 0, 6), v("P1", 0, 6), v("FD", 0, 6), OP.mult)
        cp("V", v("CBF", 0, 6), v("CB", 0, 6))
        tt(v("P1", 0, 6), v("P1", 0, 6), v("TR6", 0, 6), OP.add)
        cp("V", v("PI6", 0, 6), v("P1", 0, 6))
        ts(v("X6", 0, 6), v("PI6", 0, 6), 15, AND)
        ts(v("SI6", 0, 6), v("PI6", 0, 6), 2, SHR)
        cp("V", v("XF", 0, 6), v("X6", 0, 6))
        cp("V", v("SL", 0, 6), v("SI6", 0, 6))
        for c in range(6):
            if c % 2:
                act(v("EXB", 16 * c, 16 * c + 16), v("MASK", 0, 16), AF.Copy, scale=v("XF", c, c + 1))
            else:
                ts(v("EXB", 16 * c, 16 * c + 16), v("MASK", 0, 16), v("XF", c, c + 1), OP.mult)
        mm(v("P0", 0, 96), v("BB"), v("EXB"))
        for c in range(6):
            o = 8 * (c // 2) + c % 2, 8 * (c // 2) + 8, 2
            act(v("FIF", *o), v("F41", 0, 4), AF.Identity, bias=v("CBF", c, c + 1))
        cp("V", v("FI", 0, 24), v("FIF", 0, 24))
        ts(v("FI", 0, 24), v("FI", 0, 24), W - 1, AND)
        cp("V", v("FL", 0, 24), v("FI", 0, 24))
        for d in range(3):
            cp("A", v("FB", 128 * d, 128 * d + 128), ind(v("XR%d%d" % (rd, d)), v("FL", 8 * d, 8 * d + 8)))
        for c in range(6):
            o = 8 * (c // 2) + c % 2, 8 * (c // 2) + 8, 2
            act(v("FPF", *o), v("F4", 0, 4), AF.Identity, bias=v("P1", c, c + 1))
        ts(v("KN"), v("P0", 0, 96), p15, OP.is_le, -4.0, OP.mult)
        ts(v("CD"), v("P0", 0, 96), p15, OP.is_gt, -4.0, OP.mult)
        cp("V", ind(v("WA", 0, 1304), v("SL", 0, 6)), v("KN"))
        cp("V", ind(v("WB", 8, 1312), v("SL", 0, 6)), v("CD"))
        for s in range(2):
            o, h = (128 * s, 128 * s + 128), (512 * s, 512 * s + 512)
            init = 0.0 if s == 0 else v("P34", 511, 512)
            scan(v("P34", *h), v("WA", *h), v("WB", 512 * s + 4, 512 * s + 516), OP.add, OP.add, init)
            tt(v("SR", *o), v("P34", 512 * s + 3, 512 * s + 512, 4), v("QF", *o), OP.add)
            cp("V", v("SRL", *o), v("SR", *o))
            cp("AV"[s], v(Xn, 2048 * s, 2048 * s + 2048), ind(v("Y0"), v("SRL", *o)))
        cp("V", v("FP", 0, 24), v("FPF", 0, 24))
        cp("V", ind(v(Xn), v("FP", 0, 24)), v("FB"))
    Xn = "XA" if RO % 2 == 0 else "XB"
    for c in range(4):
        x = v(Xn, 1024 * c, 1024 * c + 1024)
        dma("SA"[c % 2], T.y[:, 1024 * c:1024 * c + 1024], ap(x), [x], [])
    for i in plan():
        now[0] = i
        ops[i][5]()
    for s in SEMAPHORES:
        if count.get(s, 0):
            wait("G", s, count[s])
